import numpy as np, ml_dtypes
CORES = [40,64,80,88,96,104,120,144]
N = 8
BF = ml_dtypes.bfloat16
def gentries(a):
    return np.ascontiguousarray(a.reshape(8, 16, -1).transpose(0, 2, 1)).reshape(8, -1)
def gtable(e):
    e = np.asarray(e); return np.ascontiguousarray(e.reshape(8, -1, 16).transpose(0, 2, 1)).reshape(128, -1).astype(np.int32)
V, L, ST, RO, CAP = 1024, 128, 2, 2, 32
W = V + RO * ST * L
E = 4095
VOID = 2 ** 20
def pack(a, c, x, t, h):
    return {"a0": np.ascontiguousarray(a.reshape(N, 128, V)).astype(np.float32).astype(BF), "kids": np.ascontiguousarray(c.reshape(N, 128, V)).astype(np.int32),
            "x0": np.ascontiguousarray(x.reshape(N, 128, L)).astype(np.float32).astype(BF), "tops": np.stack([gtable(u) for u in t]), "th": np.ascontiguousarray(h).astype(np.int32)}
def near(rng, p, n):
    k = rng.integers(0, 24, (N, 8, 1, n)); z = rng.integers(1, 25, (N, 8, 1, n))
    v = np.take_along_axis(np.broadcast_to(p, (N, 8, 16, 24)), np.broadcast_to(k, (N, 8, 16, n)), 3)
    return np.clip(v + np.rint(z * rng.standard_normal((N, 8, 16, n))), 0, 255).astype(np.int64)
def parts(rng):
    p = rng.integers(0, 256, (8, 16, 24)); p[..., ::3] = rng.integers(0, 40, (8, 16, 8))
    fill = rng.choice(np.array([0.2, 0.5, 0.8, 1.0]), (N, 8, 1, V))
    c = np.where(rng.random((N, 8, 16, V)) < fill, rng.integers(0, V, (N, 8, 16, V)), E)
    hot = np.take_along_axis(rng.integers(0, V, (N, 8, 8)), rng.integers(0, 8, (N, 8, L)), 2)
    t = np.where(rng.random((N, 8, L)) < 0.2, hot, rng.integers(0, V, (N, 8, L)))
    h = np.minimum(rng.choice(np.array([60, 200, 500, 900, 4000]), (N, 8, L)) + rng.integers(0, 100, (N, 8, L)), 4080)
    return near(rng, p, V), c, near(rng, p, L), t, h
def setup_inputs(rng):
    return pack(*parts(rng))
def setup_inputs_spread(rng):
    a = np.minimum(np.exp2(8 * rng.random((N, 8, 1, V))) * rng.random((N, 8, 16, V)), 255).astype(np.int64)
    x = np.minimum(np.exp2(8 * rng.random((N, 8, 1, L))) * rng.random((N, 8, 16, L)), 255).astype(np.int64)
    fill = np.minimum(1.25 * rng.random((N, 8, 1, V)), 1.0)
    c = np.where(rng.random((N, 8, 16, V)) < fill, np.minimum((V * rng.random((N, 8, 16, V)) ** 2).astype(np.int64), V - 1), E)
    t = np.minimum((V * rng.random((N, 8, L)) ** 3).astype(np.int64), V - 1)
    h = np.minimum(np.exp2(12 * rng.random((N, 8, L))).astype(np.int64) - 1, 4080)
    return pack(a, c, x, t, h)
def setup_inputs_ends(rng):
    def both(n):
        k = rng.integers(0, 4, (N, 8, 1, n)); m = 255 * rng.integers(0, 2, (N, 8, 16, n))
        return np.where(k == 0, 0, np.where(k == 1, 255, m))
    a, x = both(V), both(L); a[..., 0] = 255 * rng.integers(0, 2, (N, 8, 16))
    h = 4080 * rng.integers(0, 2, (N, 8, L)); s = (N, 8, 16, V)
    c = np.where(rng.random(s) < 0.5, 0, np.where(rng.random(s) < 0.3, V - 1, rng.integers(0, V, s)))
    c = np.where(rng.random(s) < rng.choice(np.array([0.1, 0.4, 0.6, 1.0]), (N, 8, 1, V)), c, E)
    m = np.argsort(rng.random((N, 8, L)), axis=2) < (2 * L) // 3
    t = np.where(m, (V - 1) * rng.integers(0, 2, (N, 8, L)), rng.integers(1, V - 5, (N, 8, L)))
    t[:, 7] = np.where(m[:, 7], t[:, 7], rng.integers(1, V - 6 - (CAP + 2), (N, L)))
    a[..., V - 1] = 255; a[..., V - 2] = 255; c[..., V - 1] = E; c[..., V - 2] = E
    c[:, :, 2, V - 1] = V - 2; c[:, :, 15, V - 1] = V - 1; c[:, :, 15, V - 2] = V - 1
    a[..., V - 5] = 0; c[..., V - 5] = E; c[:, :, 0, V - 5] = V - 5; c[..., V - 4] = V - 5
    o = t[:, 1::2]; o[o == V - 1] = 0
    for q in range(N):
        i = np.nonzero(~m[q, 7, :L - 2])[0][-(CAP + 2):]; u = V - 6 - np.arange(CAP + 2)
        c[q, 7][:, u] = V - 5; x[q, 7][:, i] = 255; h[q, 7, i] = 0; t[q, 7, i] = u
    x[..., L - 1] = 0; h[..., L - 1] = 4080; t[..., L - 1] = V - 1
    x[..., L - 2] = 255; h[..., L - 2] = 0; t[..., L - 2] = V - 4
    return pack(a, c, x, t, h)
def setup_inputs_corners(rng):
    a = rng.integers(0, 201, (N, 8, 16, V)); x = rng.integers(201, 256, (N, 8, 16, L)); s = (N, 8, 16, V)
    c = np.where(rng.random(s) < rng.choice(np.array([0.1, 0.5, 0.9]), (N, 8, 1, V)), rng.integers(0, V, s), E)
    t = np.zeros((N, 8, L), np.int64); h = np.zeros((N, 8, L), np.int64)
    case = np.array([0, 1, CAP - 1, CAP, CAP + 1, L])[rng.integers(0, 6, (N, 8))]
    case[0] = (CAP, CAP + 1, L, CAP - 1, 1, 0, CAP, CAP + 1); case[1] = (0, L, 1, 0, CAP, CAP + 1, CAP - 1, 0); case[N - 1, 7] = CAP
    for q in range(N):
        for g in range(8):
            n = int(case[q, g]); o = rng.permutation(V); full, leaf, one, more = o[:L], o[L:L + 64], o[L + 64:L + 128], o[L + 128:]; k = c[q, g]
            k[:, full] = rng.integers(0, V, (16, L)); k[:, leaf] = E; k[:, one] = E; k[rng.integers(0, 16, 64), one] = rng.integers(0, V, 64)
            if n == 0: k[15, np.all(k == E, axis=0)] = V - 1
            w = rng.integers(0, 4, L); again = rng.choice(full[:n] if n else one, L)
            u = np.where(w == 0, again, np.where(w == 1, rng.choice(leaf, L), np.where(w == 2, rng.choice(one, L), rng.choice(more, L))))
            y = np.where((w == 0) & (n > 0), 0, 4080); i = rng.permutation(L)[:n]; u[i] = full[:n]; y[i] = 0
            t[q, g] = u; h[q, g] = y
    return pack(a, c, x, t, h)
def half(rng, who, n):
    return np.where(rng.random((16, n)) < 0.5, rng.choice(who, (16, n)), E)
def late(rng, A, C, X, T, H):
    u = rng.permutation(V)[:L // 2]; A[:] = rng.integers(0, 201, (16, V)); X[:] = rng.integers(201, 256, (16, L))
    C[:, u] = rng.integers(0, V, (16, L // 2)); C[rng.integers(0, 16, L // 2), u] = E
    T[:] = np.repeat(u, 2); H[:] = 0
def splits(rng, A, C, X, T, H):
    o = rng.permutation(V); s, b, d, far = o[:L], o[L:L + 16], o[L + 16:L + 32], o[L + 32:]
    A[:, far] = rng.integers(240, 256, (16, far.size)); A[:, b] = rng.integers(200, 211, (16, 16)); A[:, d] = rng.integers(100, 121, (16, 16))
    kb = rng.integers(0, 16, 16); kd = (kb + rng.integers(1, 16, 16)) & 15; w = rng.integers(0, 16, L)
    C[:] = E; C[:, far] = half(rng, far, far.size); C[:, b] = half(rng, far, 16); C[kb, b] = E; C[kd, b] = d
    C[:, s] = half(rng, far, L); C[kd[w], s] = rng.choice(far, L); C[kb[w], s] = b[w]
    X[:] = A[:, d[w]] + rng.integers(0, 3, (16, L)); T[:] = s; H[:] = rng.integers(400, 600, L)
def hosts(rng, A, C, X, T, H):
    o = rng.permutation(V); s, b, far = o[:L], o[L:2 * L], o[2 * L:]
    X[:] = rng.integers(100, 121, (16, L)); A[:, far] = rng.integers(240, 256, (16, far.size)); A[:, b] = X + rng.integers(5, 13, (16, L))
    C[:] = E; C[:, far] = half(rng, far, far.size); C[:, b] = half(rng, far, L); C[:, s] = half(rng, far, L); C[rng.integers(0, 16, L), s] = b
    T[:] = s; H[:] = rng.integers(900, 1100, L)
def made(rng, A, C, X, T, H):
    k = L // 8; o = rng.permutation(V); v, b, s, far = o[:k], o[k:2 * k], o[2 * k:3 * k], o[3 * k:]
    i = rng.permutation(L); pz = np.sort(i[:2 * k].reshape(k, 2), axis=1); p, z, r = pz[:, 0], pz[:, 1], i[2 * k:3 * k]
    n = rng.integers(12, 41, k); m = np.argsort(rng.random((16, k)), axis=0) < 8
    w = np.argsort(rng.random((16, k)), axis=0)[:3]; w[:2] = np.sort(w[:2], axis=0)
    A[:, far] = rng.integers(240, 256, (16, far.size)); A[:, b] = np.where(m, n, 0); A[:, s] = np.where(m, n, 2 * n)
    C[:] = E; C[:, far] = half(rng, far, far.size); C[w[0], v] = b; C[w[1], v] = s
    C[:, b] = rng.choice(far, (16, k)); C[w[2], b] = E
    T[:] = rng.choice(far, L); T[p] = v; T[z] = v; T[r] = b
    y = np.where(m, 2 * n, n); X[:, p] = y; X[:, z] = n; X[:, r] = y + rng.integers(1, 4, (16, k))
    H[p] = 12 * n; H[z] = 0; H[r] = 0
def setup_inputs_ties(rng):
    a = 100 * (rng.random((N, 8, 1, V)) < 0.6) + rng.integers(0, 3, (N, 8, 16, V)) * (rng.random((N, 8, 1, V)) < 0.8)
    x = 100 + rng.integers(0, 3, (N, 8, 16, L)) * (rng.random((N, 8, 1, L)) < 0.8); s = (N, 8, 16, V)
    c = np.where(rng.random(s) < 0.5, rng.integers(0, 64, s), rng.integers(0, V, s))
    c = np.where(rng.random(s) < rng.choice(np.array([0.2, 0.6, 0.9, 1.0]), (N, 8, 1, V)), c, E)
    h = np.where(rng.random((N, 8, L)) < 0.8, rng.integers(0, 20, (N, 8, L)), 1600)
    t = rng.integers(0, V, (N, 8, L))
    for q in range(N):
        for g, fn in ((1, late), (2, splits), (4, hosts), (6, made)):
            if g == 1 or q % 2 == 0: fn(rng, a[q, g], c[q, g], x[q, g], t[q, g], h[q, g])
    return pack(a, c, x, t, h)
def setup_inputs_alike(rng):
    a, c, x, t, h = parts(rng)
    c[:, 0] = rng.integers(0, V, (N, 1, V)); c[:, 1] = np.where(c[:, 1] == E, E, np.arange(V))
    t[:, 2] = rng.integers(0, V, (N, 1)); t[:, 3] = np.where(rng.random((N, L)) < 0.5, rng.integers(0, V, (N, 1)), V - 1)
    c[:, 4] = np.where(c[:, 4] == E, E, rng.choice(np.array([0, 5, V - 1]), (N, 16, V)))
    a[:, 5] = np.minimum(a[:, 5], 200); c[:, 5] = rng.integers(0, V, (N, 16, V)); t[:, 5] = np.arange(L) % CAP
    x[:, 5] = rng.integers(201, 256, (N, 16, L)); h[:, 5] = 0
    x[:, 6] = x[:, 6, :, :1]
    c[:, 7] = rng.integers(0, V, (N, 16, V))
    return pack(a, c, x, t, h)
def check_inputs(d):
    bad = []
    for k, lo, hi in (("a0", 0, 255), ("kids", 0, E), ("x0", 0, 255), ("tops", 0, V - 1), ("th", 0, 4080)):
        v = np.asarray(d[k]).astype(np.float64)
        if not (np.min(v) >= lo and np.max(v) <= hi) or np.any(v != np.floor(v)): bad.append("range of " + k)
        elif k == "kids" and np.any((v >= V) & (v != E)): bad.append("range of " + k)
    return bad
def first(key, on):
    k = np.where(on, key, 8192 + np.arange(L)); o = np.argsort(k, axis=1, kind="stable"); s = np.take_along_axis(k, o, 1)
    m = np.ones(k.shape, bool); m[:, 1:] = s[:, 1:] != s[:, :-1]
    r = np.zeros(k.shape, bool); np.put_along_axis(r, o, m, 1)
    return r & on
def pick(t, i):
    return t[np.arange(t.shape[0]).reshape((-1,) + (1,) * (i.ndim - 1)), i]
def at(t, k):
    return np.take_along_axis(t, k[..., None], 2)[..., 0]
def reference(a0, kids, x0, tops, th):
    B = 8 * N
    A = np.zeros((B, W, 16), np.int32); A[:, :V] = a0.astype(np.float32).astype(np.int32).reshape(B, 16, V).transpose(0, 2, 1)
    C = np.full((B, W, 16), E, np.int32); C[:, :V] = kids.reshape(B, 16, V).transpose(0, 2, 1)
    x = np.ascontiguousarray(x0.astype(np.float32).astype(np.int32).reshape(B, 16, L).transpose(0, 2, 1))
    top = np.stack([gentries(u) for u in tops]).astype(np.int64).reshape(B, L); lim = th.reshape(B, L).astype(np.int32)
    for rnd in range(RO):
        v = top.copy(); rest = np.zeros((B, L), bool)
        come = np.zeros((N, 8, ST * CAP, 16), np.int32); ok = np.zeros((N, 8, ST * CAP), bool)
        for j in range(ST):
            sg = rnd * ST + j; act = first(v, ~rest)
            c = pick(C, v); filled = c != E
            e = np.where(filled, np.add.reduce(np.abs(x[:, :, None] - pick(A, np.where(filled, c, 0))), axis=3), VOID)
            kb = np.argmin(e, axis=2); eb = at(e, kb); e2 = e.copy(); np.put_along_axis(e2, kb[..., None], VOID, 2)
            kq = np.argmin(e2, axis=2); eq = at(e2, kq)
            b = np.where(eb < VOID, at(c, kb), 0); q = np.where(eq < VOID, at(c, kq), 0)
            ab = pick(A, b); mid = (ab + pick(A, q)) >> 1
            em = np.where(eq < VOID, np.add.reduce(np.abs(x - mid), axis=2), VOID)
            d = np.where((eb < VOID)[..., None], pick(C, b), E)
            f = np.where(d != E, np.add.reduce(np.abs(x[:, :, None] - pick(A, np.where(d != E, d, 0))), axis=3), VOID)
            w = np.argmin(np.stack([eb, em, np.min(f, axis=2), lim], axis=2), axis=2)
            host, merge, split, new = [act & (w == u) for u in range(4)]
            empty = ~filled; room = np.any(empty, axis=2); k0 = np.argmax(empty, axis=2); over = new & ~room
            n = V + L * sg + np.arange(L)
            g, i = np.nonzero(host & first(b, host))
            A[g, b[g, i]] = ab[g, i] + np.clip(x[g, i] - ab[g, i], -4, 4)
            g, i = np.nonzero(merge)
            A[g, n[i]] = mid[g, i]; C[g, n[i], kb[g, i]] = b[g, i]; C[g, n[i], kq[g, i]] = q[g, i]
            C[g, v[g, i], kb[g, i]] = n[i]; C[g, v[g, i], kq[g, i]] = E
            g, i = np.nonzero(split)
            t = c[g, i]; t[np.arange(len(g)), kb[g, i]] = E; C[g, v[g, i]] = np.where(t == E, d[g, i], t)
            g, i = np.nonzero(new & room)
            A[g, n[i]] = x[g, i]; C[g, v[g, i], k0[g, i]] = n[i]
            v = np.where(host, b, np.where(merge, n, v)); rest = rest | new
            pl = np.add.accumulate(over.astype(np.int64), axis=1) - 1; g, i = np.nonzero(over & (pl < CAP))
            to = (g // 8 + 1 + sg % (N - 1)) % N
            come[to, g % 8, j * CAP + pl[g, i]] = x[g, i]; ok[to, g % 8, j * CAP + pl[g, i]] = True
        ok = ok.reshape(B, ST * CAP); come = pick(come.reshape(B, ST * CAP, 16), np.argsort(~ok, axis=1, kind="stable"))
        cnt = np.add.reduce(ok.astype(np.int64), axis=1)[:, None]; nr = np.add.accumulate(rest.astype(np.int64), axis=1) - 1
        got = rest & (nr < cnt)
        x = np.where(got[..., None], pick(come, np.clip(nr, 0, ST * CAP - 1)), np.abs(x - pick(A, v)))
    return {"ya": np.ascontiguousarray(A.transpose(0, 2, 1)).reshape(N, 128, W).astype(np.float32).astype(BF),
            "yc": np.ascontiguousarray(C.transpose(0, 2, 1)).reshape(N, 128, W).astype(np.float32),
            "yx": np.ascontiguousarray(x.transpose(0, 2, 1)).reshape(N, 128, L).astype(np.float32).astype(BF)}

@@ -1,0 +1,642 @@
+from concourse.mybir import AluOpType as OP, ActivationFunctionType as AF, AxisListType
+
+V0, L, ST, RO, CAP, NR = 1024, 128, 2, 2, 32, 8
+W = V0 + RO * ST * L
+E1 = W
+WIN = W + 8
+DUMP = WIN
+FAR = 2048
+BIG = float(2 ** 30)
+MAGIC = float(2 ** 23)
+PIECES = [(0, 32), (32, 32), (64, 32), (96, 16), (112, 16)]
+
+SLOT = {}
+SIZE = {"F": 0, "B": 0, "I": 0, "U": 0}
+
+
+def _s(kind, **kw):
+    for n, w in kw.items():
+        SLOT[n] = ("ar" + kind, SIZE[kind], w)
+        SIZE[kind] += (w + 15) // 16 * 16
+
+
+_s("B", A=1680, xrep=2048, df=2048, ag=2048, ab2=2048, xb=128, xT=128, R=2048, onesb=512, zb=512, idb=128, ipb=136,
+   hc=272, f16p=136, selb=8, sel2=8, bk=16, sb=32, tri=128, trib=512, kcb=408, rmask=384, Di=128, I128=128, GN=640, GE=256,
+   PS=256, m1c=128, bb=143, bs=1664, EE=128, Tb=1664, h8=128, Fm=128, cod=128, codE=128, codO=128, bod=128, bodE=128, bodO=128,
+   eqa=1024, eqb=1024, ex=256, ex2=256, oh=384, gx=256, gm=384, exS=128, exU=128, exH=128, exP=128, exN=128, absM=128, Mb=128,
+   An=128, hv=128, hF=8, ov=8, nov=8, rest=8, rest2=8, nonr=8, nonr2=8, one8=8, nF=8, dA=128)
+_s("F", C=3840, idf=136, zf=272, RM=272, RM2=128, kcf=408, kcg=408, kpat=384, iGL=8, dmp=8, lim=8, lim1=8, thf=128, topf=8,
+   r=128, y=128, cvf=128, dvf=128, m1=272, m2=272, cand=272, k0s=136, k031=8, abm=128, sm=128, ym=128, xs=128, xp=128, dM=128,
+   hm=8, he=8, nn=8, T0=8, Tt=8, act0=8, act1=8, an=8, ah0=8, gk=24, kk=24, k1=8, k2=8, wal=128, ral=128, w3=128, f3=128, t3=128,
+   rsp=128, c0=128, cb=128, t1=128, t2=128, am2=16, X3=24, g3=24, gm3=32, Dv=16, Bv=16, q1=16, vf=16, bf=8, fsm=128, Sf=8, anr0=8, nrm=8, h1=8,
+   oA=8, pos=8, nrs=8, hd=128, hc1=128, ge=8, idx=8, msk=32, n0=1, cd=1, ad=128, mE=1, mO=1, nv=8, bd=8, p128=1)
+_s("I", KI=1024, tp=8, thi=128, ci=128, rmi=384, pin=8, pr=8, m16=8, cio=13, bt=143, m1e=16, dec=16, eb=8, kb=8, m2e=16,
+   dec2=16, kq=8, hx=128, xi=128, iv=8, ip=8)
+_s("U", bl=128, tu=8, cvu=128, dvu=128, bu=8, qu=8, uvu=8, vu2=16, oAu=8, posu=8, iu=8)
+
+SCRATCH = {"arF": ("sbuf", [128, SIZE["F"]], "float32"), "arB": ("sbuf", [128, SIZE["B"]], "bfloat16"),
+           "arI": ("sbuf", [128, SIZE["I"]], "int32"), "arU": ("sbuf", [128, SIZE["U"]], "uint16")}
+for _k in range(8):
+    SCRATCH["pb%d" % _k] = ("psum", [128, 512], "float32")
+for _k in range(4):
+    SCRATCH["msg%d" % _k] = ("sbuf", [128, 256], "float32")
+    SCRATCH["rl%d" % _k] = ("sbuf", [128, 32], "float32")
+for _k in range(2):
+    SCRATCH["come%d" % _k] = ("sbuf", [128, 80], "float32")
+SEMAPHORES = (["qv", "qs", "qt", "qg"] + ["in%d" % k for k in range(4)] + ["rr%d" % k for k in range(4)] + ["ls%d" % k for k in range(4)]
+              + ["ld%d" % k for k in range(8)])
+
+
+def emask(topo, src, dst, n):
+    m = 0
+    for e in topo.engines(src, dst)[:n]:
+        m |= 1 << e
+    return m
+
+
+NE_ON, NE_OFF = 8, 8
+
+
+def hops(T, topo, rank, s):
+    src, dst = T.cores[rank], T.cores[(rank + 1 + s % (NR - 1)) % NR]
+    if s > 0 and topo.may_write(src, dst):
+        return [src, dst]
+    ways = [c for c in topo.cores_of(src) if c != src and all(topo.may_write(c, d) for d in T.cores if d not in topo.cores_of(src))]
+    ways.sort(key=lambda c: topo.die(c) != topo.die(src))
+    return [src, ways[0], dst]
+
+
+def engines_of(topo, a, b):
+    return NE_ON if b in topo.cores_of(a) else NE_OFF
+
+
+def relay(g, core, T, topo):
+    for s in range(ST * RO):
+        for rank in range(NR):
+            h = hops(T, topo, rank, s)
+            if len(h) == 3 and h[1] == core:
+                n = engines_of(topo, h[1], h[2])
+                g.wait_ge(T.sem["rr%d" % s], engines_of(topo, h[0], core))
+                rid, pid = topo.addr(h[2], core)
+                g.remote_dma(T["come%d" % (s // ST)][:, CAP * (s % ST):CAP * (s % ST) + CAP], T["rl%d" % s][:, 0:CAP], T.sem["in%d" % s],
+                             T.sem["ls%d" % s], pid, rid, emask(topo, core, h[2], n))
+    for s in range(ST * RO):
+        for rank in range(NR):
+            h = hops(T, topo, rank, s)
+            if len(h) == 3 and h[1] == core:
+                g.wait_ge(T.sem["ls%d" % s], engines_of(topo, h[1], h[2]))
+
+
+def rank_program(g, core, T, topo):
+    rank = T.rank_of(core)
+    if rank is None:
+        relay(g, core, T, topo)
+        return
+    eng = {"v": g.vector, "s": g.scalar, "t": g.tensor, "g": g, "y": g.sync}
+    own = {"v": "qv", "s": "qs", "t": "qt", "g": "qg"}
+    cnt = {"qv": 0, "qs": 0, "qt": 0, "qg": 0}
+    know = {q: {} for q in eng}
+    wr, rd = {}, {}
+
+    def need(q, R, Wk, dma=False):
+        deps = []
+        for k in R:
+            if k in wr:
+                deps.append(wr[k])
+            if k[:2] == "pb":
+                deps += [d for d in rd.get(k, []) if d[0] != q]
+        for k in Wk:
+            if k in wr and (wr[k][0] != q or dma):
+                deps.append(wr[k])
+            deps += [d for d in rd.get(k, []) if d[0] != q or dma]
+        deps = sorted(deps, key=lambda d: -d[2])
+        for d in deps:
+            if know[q].get(d[1], 0) < d[2]:
+                eng[q].wait_ge(T.sem[d[1]], d[2])
+                for n, v in d[3].items():
+                    know[q][n] = max(know[q].get(n, 0), v)
+
+    def note(tag, sem, val, snap, R, Wk):
+        snap = dict(snap)
+        snap[sem] = val
+        d = (tag, sem, val, snap)
+        for k in R:
+            rd.setdefault(k, []).append(d)
+            rd[k] = [e for e in rd[k] if e is d or e[0] != tag or e[1] != sem]
+        for k in Wk:
+            wr[k] = d
+            rd[k] = []
+
+    def op(q, call, R, Wk):
+        need(q, R, Wk)
+        s = own[q]
+        cnt[s] += 1
+        call(eng[q]).then_inc(T.sem[s], 1)
+        note(q, s, cnt[s], know[q], R, Wk)
+
+    def dma(q, sem, out, in_, R, Wk):
+        need(q, R, Wk, True)
+        eng[q].dma_start(out, in_).then_inc(T.sem[sem], 16)
+        cnt[sem] = 16
+        note("dma" + sem, sem, 16, know[q], R, Wk)
+
+    def b(name, c0=0, c1=None, st=1, p0=0, p1=128, key=None):
+        if name in SLOT:
+            buf, o, w = SLOT[name]
+        else:
+            buf, o, w = name, 0, SCRATCH[name][1][1]
+        c1 = w if c1 is None else c1
+        return (T[buf][p0:p1, o + c0:o + c1:st] if st != 1 else T[buf][p0:p1, o + c0:o + c1], [key or name])
+
+    def ind(win, off):
+        return (win[0].indirect(off[0]), win[1] + off[1])
+
+    def ks(*refs):
+        return [k for r in refs if isinstance(r, tuple) for k in r[1]]
+
+    def split_out(o):
+        return (o[1][1:] if len(o[1]) > 1 else []), o[1][:1]
+
+    def ap(x):
+        return x[0] if isinstance(x, tuple) else x
+
+    def tt(o, a, c, f):
+        op("v", lambda e: e.tensor_tensor(o[0], a[0], c[0], f), ks(a, c), ks(o))
+
+    def ts(o, a, s1, f0, s2=None, f1=None):
+        if f1 is None:
+            op("v", lambda e: e.tensor_scalar(o[0], a[0], ap(s1), None, f0), ks(a, s1), ks(o))
+        else:
+            op("v", lambda e: e.tensor_scalar(o[0], a[0], ap(s1), ap(s2), f0, f1), ks(a, s1, s2), ks(o))
+
+    def cp(o, a):
+        r, w = split_out(o)
+        op("v", lambda e: e.tensor_copy(o[0], a[0]), ks(a) + r, w)
+
+    def ms(o, v):
+        op("v", lambda e: e.memset(o[0], v), [], ks(o))
+
+    def scan(o, a, c, f0, f1):
+        op("v", lambda e: e.tensor_tensor_scan(o[0], a[0], c[0], BIG, f0, f1), ks(a, c), ks(o))
+
+    def act(o, a, f, bias=0.0, scale=1.0):
+        op("s", lambda e: e.activation(o[0], a[0], f, bias=bias, scale=ap(scale)), ks(a, scale), ks(o))
+
+    def mm(o, l, r, start=True, stop=True):
+        op("t", lambda e: e.matmul(o[0], l[0], r[0], start, stop), ks(l, r), ks(o))
+
+    def io(o, pat, base, cm, flag=False):
+        if flag:
+            op("g", lambda e: e.iota(o[0], pat, base, cm, allow_small_or_imprecise_dtypes=True), [], ks(o))
+        else:
+            op("g", lambda e: e.iota(o[0], pat, base, cm), [], ks(o))
+
+    def asel(o, a, pat, f, fill, base, cm):
+        op("g", lambda e: e.affine_select(o[0], a[0], pat, f, fill, base, cm), ks(a), ks(o))
+
+    bl = lambda n, c0=0: b("bl", c0, c0 + n)
+
+    ms(b("A", V0, W), 0.0)
+    ms(b("A", W, WIN), 4096.0)
+    dma("y", "ld0", b("tp")[0], T.tops[:], [], ["tp"])
+    dma("y", "ld1", b("xb")[0], T.x0[:], [], ["xb"])
+    dma("y", "ld2", b("KI")[0], T.kids[:], [], ["KI"])
+    dma("y", "ld3", b("A", 0, V0)[0], T.a0[:], [], ["A"])
+    dma("s", "ld4", b("thi", 0, 128, 1, 0, 8)[0], T.th[:], [], ["thi"])
+
+    ms(b("onesb"), 1.0)
+    ms(b("zf"), 0.0)
+    io(b("ci"), [[1, 128]], 0, 0)
+    cp(b("bl"), b("ci"))
+    cp(b("tu"), b("tp"))
+    cp(b("topf"), b("tp"))
+    for k in range(16):
+        cp(b("xrep", k, 2048, 16, key="xr"), b("xb"))
+    ms(b("C", V0, WIN), 4095.0)
+    asel(b("idb"), b("onesb", 0, 128), [[-1, 128]], OP.is_equal, 0.0, 0, 1)
+    asel(b("ipb"), b("onesb", 0, 136), [[-16, 8], [-1, 17]], OP.is_equal, 0.0, 1, 1)
+    io(b("kcf", 0, 136, key="kcf0"), [[0, 8], [128, 17]], -64, 0, True)
+    io(b("kcf", 136, 272, key="kcf1"), [[0, 8], [128, 17]], -128, 0, True)
+    io(b("kcf", 272, 408, key="kcf2"), [[0, 8], [1, 17]], -1, 0, True)
+    op("g", lambda e: e.affine_select(b("kcg")[0], b("kcf")[0], [[0, 24], [1, 17]], OP.not_equal, BIG, 0, 0), ["kcf0", "kcf1", "kcf2"], ["kcg"])
+    asel(b("sel2"), b("onesb", 0, 8), [[-16, 8]], OP.is_ge, 0.0, 0, 1)
+    asel(b("selb"), b("sel2"), [[16, 8]], OP.is_ge, 0.0, 15, -1)
+    asel(b("RM"), b("zf"), [[0, 16], [1, 17]], OP.not_equal, BIG, 0, 0)
+    io(b("rmi"), [[0, 24], [-1, 16]], 16, 1)
+    io(b("cio"), [[128, 13]], 0, 1)
+    ms(b("R"), -1.0)
+    asel(b("R"), b("R"), [[-1, 128], [0, 16]], OP.is_equal, 0.0, 0, 1)
+    io(b("pin"), [[0, 8]], 0, 1)
+    io(b("m16"), [[16, 8]], 0, 0)
+    io(b("kpat"), [[0, 24], [1, 16]], -31, 0, True)
+    ms(b("zb"), 0.0)
+    asel(b("EE", p1=16), b("onesb", 0, 128, 1, 0, 16), [[0, 8], [-1, 16]], OP.is_equal, 0.0, 0, 1)
+    asel(b("trib"), b("zb"), [[0, 4], [1, 128]], OP.is_gt, -32.0, 0, -1)
+    asel(b("tri"), b("onesb", 0, 128), [[1, 128]], OP.is_gt, 0.0, 0, -1)
+    asel(b("RM2"), b("zf", 0, 128), [[0, 8], [1, 16]], OP.not_equal, BIG, 0, 0)
+    for k in range(4):
+        io(b("msg%d" % k, 0, CAP), [[0, CAP]], 0, 0, True)
+    for k in range(2):
+        io(b("come%d" % k, 64, 80, key="come%dz" % k), [[0, 16]], 0, 0, True)
+
+    def consts_a():
+        cp(b("idf"), b("ipb"))
+        ts(b("hc", 0, 136, key="hc0"), b("ipb"), -16.0, OP.mult)
+        cp(b("hc", 136, 272, key="hc1"), b("ipb"))
+        ts(b("f16p"), b("ipb"), 16.0, OP.mult)
+        cp(b("kcb"), b("kcg"))
+        ts(b("bk", 0, 8, key="bk0"), b("selb"), 2048.0, OP.mult)
+        ts(b("bk", 8, 16, key="bk1"), b("selb"), 2048.0, OP.mult)
+
+    def consts_b():
+        for j, m in enumerate((-1.0, -16.0, 1.0, -2048.0)):
+            ts(b("sb", 8 * j, 8 * j + 8, key="sb%d" % j), b("selb"), m, OP.mult)
+        ts(b("rmi"), b("rmi"), 15, OP.bitwise_and)
+        ts(b("rmask"), b("rmi"), 0.0, OP.is_equal)
+
+    def consts_c():
+        ms(b("one8"), 1.0)
+        cp(b("thf", 0, 128, 1, 0, 8), b("thi", 0, 128, 1, 0, 8))
+        mm(b("pb3", 0, 8), b("thf", 0, 128, 1, 0, 8), b("idf", 1, 9, 1, 0, 8))
+        cp(b("lim"), b("pb3", 0, 8))
+        ts(b("lim1"), b("lim"), 1.0, OP.add)
+        ts(b("pr"), b("pin"), 15, OP.bitwise_and)
+        tt(b("iGL"), b("pr"), b("m16"), OP.add)
+        ts(b("dmp"), b("iGL"), float(DUMP), OP.add)
+        for k in range(11):
+            ts(b("bt", 13 * k, 13 * k + 13, key="bt"), b("cio"), k, OP.logical_shift_right, 1, OP.bitwise_and)
+        ts(b("bb"), b("bt"), 2.0, OP.mult, -1.0, OP.add)
+        for q in range(13):
+            mm(b("pb%d" % (4 + q // 4), 128 * (q % 4), 128 * (q % 4) + 128, 1, 0, 11), b("bb", q, 143, 13), b("idb"))
+        for h in range(4):
+            n = 512 if h < 3 else 128
+            act(b("bs", 512 * h, 512 * h + n, 1, 0, 11, key="bs%d" % h), b("pb%d" % (4 + h), 0, n, 1, 0, 11), AF.Copy)
+        for h in range(4):
+            n = 512 if h < 3 else 128
+            mm(b("pb%d" % (4 + h), 0, n), b("EE", p1=11), b("bs", 512 * h, 512 * h + n, 1, 0, 11, key="bs%d" % h))
+            act(b("Tb", 512 * h, 512 * h + n), b("pb%d" % (4 + h), 0, n), AF.Copy)
+        ts(b("iv"), b("pin"), 4, OP.logical_shift_right, 1, OP.bitwise_and)
+        cp(b("mO"), b("iv", 0, 1))
+        ts(b("mE"), b("iv", 0, 1), -1.0, OP.mult, 1.0, OP.add)
+
+    def consts_d():
+        tt(b("Di"), b("idb"), b("ci"), OP.mult)
+        ts(b("I128"), b("idb"), 128.0, OP.mult)
+        ts(b("p128"), b("pin", 0, 1), 128.0, OP.add)
+        ts(b("GN", 0, 128, key="GNa"), b("idb"), 8192.0, OP.mult)
+        for s in range(4):
+            ts(b("GN", 128 + 128 * s, 256 + 128 * s, key="GN%d" % s), b("idb"), float(128 * (s - 56)), OP.mult)
+        ts(b("GE", 0, 128, key="GE0"), b("idb"), -4096.0, OP.mult)
+        ts(b("GE", 128, 256, key="GE1"), b("idb"), 4096.0, OP.mult)
+        ts(b("m1c"), b("idb"), -1.0, OP.mult)
+
+    def x_forms(src):
+        ts(b("xs"), src, MAGIC, OP.add)
+        ts(b("xp"), src, 256.0, OP.add)
+
+    def turn_x():
+        mm(b("pb3", 0, 128), b("xb"), b("idb"))
+        act(b("xT"), b("pb3", 0, 128), AF.Copy)
+
+    def preload_x():
+        for c in range(4):
+            mm(b("pb%d" % (4 + c)), b("xT"), b("R", 512 * c, 512 * c + 512), True, False)
+
+    def codes(u, d):
+        act(b(d), ind(b("Tb", 0, WIN), u), AF.Copy)
+        act(b(d + "E"), b(d), AF.Copy, 0.0, b("mE"))
+        act(b(d + "O"), b(d), AF.Copy, 0.0, b("mO"))
+
+    def equal(d, banks, out):
+        for h in range(2):
+            bank = banks[h]
+            mm(b(bank), b("idb"), b("trib"), True, False)
+            for j in range(4):
+                w = 4 * h + j
+                p = w // 2 * 32
+                if j == 2:
+                    need("t", [bank], [])
+                mm(b(bank, 128 * j, 128 * j + 128), b(d, 0, 128, 1, p, p + 32), b(d + ("O" if w % 2 else "E"), 0, 128, 1, p, p + 32),
+                   False, j == 3)
+            act(b(out, 512 * h, 512 * h + 512, key=out + str(h)), b(bank), AF.Relu, -10.0)
+
+    def count(eq, mask, o):
+        for w in range(8):
+            mm(b(o[0], o[1] + w, o[1] + w + 1), b(eq, 128 * w, 128 * w + 128, key=eq + str(w // 4)), b(mask, w, w + 1))
+
+    def to_lists(ex, n, o, scales):
+        for j in range(n):
+            mm(b(o[0], o[1] + 8 * j, o[1] + 8 * j + 8), b(ex, 128 * j, 128 * j + 128), b("sb", 8 * scales[j], 8 * scales[j] + 8, key="sb%d" % scales[j]))
+
+    def expand(ex, src, n):
+        tt(b(ex, 0, 128 * n), ind(src, bl(8 * n)), b("rmask", 0, 128 * n), OP.mult)
+
+    def front(s, vu):
+        if s == 0:
+            ts(b("cvu"), ind(b("KI"), vu), float(E1), OP.min)
+            cp(b("C", 0, V0), b("KI"))
+        else:
+            ts(b("cvu"), ind(b("C", 0, WIN), vu), float(E1), OP.min)
+        act(b("r"), ind(b("C", 0, WIN), vu), AF.Relu, float(E1), -1.0)
+        act(b("y"), b("r"), AF.Identity, MAGIC, 1.0 / 127.95)
+        act(b("h8"), b("y"), AF.Identity, -8 * MAGIC, 8.0)
+        act(b("Fm"), b("r"), AF.Sign)
+        if s == 0:
+            consts_a()
+        one = b("onesb", 0, 128, 1, 0, 1)
+        mm(b("pb0", 272, 408), one, b("kcb", 272, 408, 1, 0, 1), True, False)
+        mm(b("pb0", 272, 408), b("Fm"), b("f16p"), False, True)
+        mm(b("pb0", 0, 272), one, b("kcb", 0, 272, 1, 0, 1), True, False)
+        mm(b("pb0", 0, 136), b("r"), b("idf"), False, False)
+        op("t", lambda e: e.matmul(b("pb0", 0, 272)[0], b("h8")[0], b("hc")[0], False, False), ["h8", "hc0", "hc1"], ["pb0"])
+
+    act_name = {0: "act0", 1: "act1", 2: "act0", 3: "act1"}
+
+    def step(s, vu, vf):
+        t = s % ST
+        rnd = s // ST
+        n0 = V0 + L * s
+        if s != 2:
+            front(s, vu)
+        if s == 0:
+            x_forms(b("xb"))
+            turn_x()
+        if t == 1:
+            codes(vu, "cod")
+        if t == 1:
+            preload_x()
+        for j, (l0, n) in enumerate(PIECES):
+            c0, c1 = 16 * l0, 16 * (l0 + n)
+            if s == 2:
+                tt(b("df", c0, c1, key="df%d" % j), ind(b("xi"), bl(n, l0)), b("ag", c0, c1, key="ag%d" % (l0 // 32)), OP.subtract)
+                if j == 0:
+                    cp(b("xb"), b("xi"))
+                    turn_x()
+                    preload_x()
+            else:
+                op("v", lambda e: e.tensor_tensor(b("df", c0, c1)[0], ind(b("A", 0, WIN), b("cvu", l0, l0 + n))[0], b("xrep", c0, c1)[0], OP.subtract),
+                   ["A", "cvu", "xr"], ["df%d" % j])
+            act(b("df", c0, c1, key="df%d" % j), b("df", c0, c1, key="df%d" % j), AF.Abs)
+        for l0, l1, js in ((0, 96, (0, 1, 2)), (96, 128, (3, 4))):
+            for k in range(16):
+                op("t", lambda e: e.matmul(b("pb0", 1 + k, 272, 17, l0, l1)[0], b("df", 16 * l0 + k, 16 * l1, 16)[0], b("bk")[0], False, k == 15),
+                   ["df%d" % j for j in js] + ["bk0", "bk1"], ["pb0"])
+        if s == 0:
+            consts_b()
+        if s == 2:
+            x_forms(b("xi"))
+        scan(b("m1"), b("RM"), b("pb0", 0, 272), OP.max, OP.min)
+        cp(b("m1e"), b("m1", 16, 272, 17))
+        ts(b("dec"), b("m1e"), 127, OP.bitwise_and)
+        expand("ex", b("dec"), 2)
+        scan(b("k0s"), b("RM", 0, 136), b("pb0", 272, 408), OP.max, OP.min)
+        to_b = b("pb1", 0, 8)
+        mm(to_b, b("ex", 0, 128), b("sb", 0, 8, key="sb0"), True, False)
+        mm(to_b, b("ex", 128, 256), b("sb", 8, 16, key="sb1"), False, True)
+        ts(b("bu"), to_b, 1600.0, OP.add)
+        ts(b("dvu"), ind(b("C", 0, WIN), b("bu")), float(E1), OP.min)
+        ts(b("bf"), to_b, 1600.0, OP.add)
+        act(b("cvf"), ind(b("C", 0, WIN), vu), AF.Copy)
+        act(b("abm"), ind(b("A", 0, WIN), b("bu")), AF.Identity, -0.5)
+        if s == 0:
+            consts_c()
+            codes(b("tu"), "cod")
+            preload_x()
+        if t == 1 or s == 0:
+            equal("cod", ("pb2", "pb3"), "eqa")
+        op("v", lambda e: e.tensor_tensor(b("cand", 1, 272)[0], b("m1", 0, 271)[0], b("pb0", 1, 272)[0], OP.max), ["m1", "pb0"], ["cand"])
+        op("v", lambda e: e.tensor_tensor_scan(b("m2", 1, 272)[0], b("RM", 1, 272)[0], b("cand", 1, 272)[0], BIG, OP.max, OP.min), ["RM", "cand"], ["m2"])
+        cp(b("m2e"), b("m2", 16, 272, 17))
+        ts(b("dec2"), b("m2e"), 127, OP.bitwise_and)
+        expand("ex2", b("dec2"), 2)
+        to_q = b("pb1", 8, 16)
+        mm(to_q, b("ex2", 0, 128), b("sb", 0, 8, key="sb0"), True, False)
+        mm(to_q, b("ex2", 128, 256), b("sb", 8, 16, key="sb1"), False, True)
+        ts(b("eb"), b("m1e", 0, 8), 11, OP.logical_shift_right)
+        ts(b("kb"), b("m1e", 0, 8), 7, OP.logical_shift_right, 15, OP.bitwise_and)
+        ts(b("kq"), b("m2e", 0, 8), 7, OP.logical_shift_right, 15, OP.bitwise_and)
+        ts(b("qu"), to_q, 1600.0, OP.add)
+        tt(b("sm"), ind(b("A", 0, WIN), b("qu")), b("abm"), OP.add)
+        ts(b("ym"), b("sm"), 0.5, OP.mult, MAGIC, OP.add)
+        tt(b("dM"), b("xs"), b("ym"), OP.subtract)
+        def gather(c):
+            act(b("ag", 512 * c, 512 * c + 512, key="ag%d" % c), ind(b("A", 0, WIN), b("dvu", 32 * c, 32 * c + 32)), AF.Copy)
+            mm(b("pb%d" % (4 + c)), b("idb"), b("ag", 512 * c, 512 * c + 512, key="ag%d" % c), False, True)
+
+        def away(c):
+            act(b("ab2", 512 * c, 512 * c + 512, key="ab2%d" % c), b("pb%d" % (4 + c)), AF.Abs)
+
+        gather(0)
+        gather(1)
+        away(0)
+        if t == 1 or s == 0:
+            count("eqa", "nonr" if t == 1 else "one8", ("pb1", 16))
+        gather(2)
+        act(b("absM"), b("dM"), AF.Abs)
+        act(b("Mb"), b("ym"), AF.Identity, -MAGIC)
+        mm(b("pb1", 24, 32), b("absM"), b("selb"))
+        act(b("dvf"), ind(b("C", 0, WIN), b("bu")), AF.Copy)
+        away(1)
+        gather(3)
+        away(2)
+
+        ac = act_name[s]
+        if s == 0 or t == 1:
+            tt(b(ac), b("pb1", 16, 24), b("one8" if s == 0 else "nonr"), OP.is_lt)
+        em = b("pb1", 24, 32)
+        tt(b("hm"), em, b("eb"), OP.min)
+        tt(b("he"), em, b("eb"), OP.is_ge)
+        ts(b("k031"), b("k0s", 16, 136, 17), -31.0, OP.add)
+        tt(b("nn"), b("lim"), b("hm"), OP.is_lt)
+        tt(b("T0"), b("lim1"), b("hm"), OP.min)
+        tt(b("an"), b("nn"), b(ac), OP.mult)
+        tt(b("Tt"), b("T0"), b(ac), OP.mult)
+        tt(b("ah0"), b(ac), b("an"), OP.subtract)
+        ts(b("nrm"), b("k031"), -15.0, OP.is_ge)
+        tt(b("gm3", 0, 8, key="ah"), b("ah0"), b("he"), OP.mult)
+        ts(b("kk", 0, 8, key="kk0"), b("kb"), -31.0, OP.add)
+        tt(b("anr0"), b("an"), b("nrm"), OP.mult)
+        tt(b("gm3", 16, 24, key="am"), b("ah0"), b("gm3", 0, 8, key="ah"), OP.subtract)
+        ts(b("nv"), b("kq"), -31.0, OP.add)
+        tt(b("k2"), b("an"), b("k031"), OP.mult)
+        tt(b("k1"), b("gm3", 16, 24, key="am"), b("kk", 0, 8, key="kk0"), OP.mult)
+        tt(b("kk", 16, 24, key="kk2"), b("gm3", 16, 24, key="am"), b("nv"), OP.mult)
+        tt(b("kk", 8, 16, key="kk1"), b("k1"), b("k2"), OP.add)
+        tt(b("gm3", 24, 32, key="ax"), b("an"), b("anr0"), OP.subtract)
+        cp(b("gm3", 8, 16, key="ac"), b(ac))
+        op("v", lambda e: e.tensor_tensor(b("oh")[0], ind(b("kk"), bl(24))[0], b("kpat")[0], OP.is_equal), ["kk0", "kk1", "kk2", "bl", "kpat"], ["oh"])
+        if s == 0:
+            consts_d()
+        ohb, ohn, ohe = b("oh", 0, 128), b("oh", 128, 256), b("oh", 256, 384)
+        i8 = b("GN", 0, 128, key="GNa")
+        mm(b("pb2", 0, 128), ohn, i8, True, False)
+        mm(b("pb2", 0, 128), ohe, i8, False, True)
+        mm(b("pb2", 128, 256), ohn, b("GN", 128 + 128 * s, 256 + 128 * s, key="GN%d" % s), True, False)
+        mm(b("pb2", 128, 256), ohn, b("Di"), False, False)
+        mm(b("pb2", 128, 256), ohe, b("GE", 0, 128, key="GE0"), False, False)
+        mm(b("pb2", 128, 256), ohe, b("m1c"), False, True)
+        mm(b("pb2", 256, 384), ohb, i8)
+        op("v", lambda e: e.tensor_tensor(b("gm")[0], ind(b("gm3", 0, 24), bl(24))[0], b("rmask")[0], OP.mult), ["ah", "am", "ac", "bl", "rmask"], ["gm"])
+        to_lists("gm", 3, ("pb1", 32), (2, 2, 2))
+        away(3)
+        op("s", lambda e: e.activation(b("gx")[0], ind(b("gm3", 16, 32), bl(16))[0], AF.Copy, bias=0.0, scale=1.0), ["am", "ax", "bl"], ["gx"])
+        for l0, l1, cs in ((0, 96, (0, 1, 2)), (96, 128, (3,))):
+            for k in range(16):
+                op("t", lambda e: e.matmul(b("pb0", k, 128, 16, l0, l1)[0], b("ab2", 16 * l0 + k, 16 * l1, 16)[0], b("selb")[0], True, True),
+                   ["ab2%d" % c for c in cs] + ["selb"], ["pb0"])
+        codes(b("bu"), "bod")
+        tt(b("wal"), b("cvf"), b("pb2", 0, 128), OP.max)
+        tt(b("ral"), b("wal"), b("pb2", 128, 256), OP.add)
+        tt(b("w3"), b("cvf"), b("pb2", 256, 384), OP.max)
+        ts(b("c0"), b("pb2", 0, 128), 0.0, OP.is_equal, 4095.0, OP.mult)
+        mm(b("pb3", 0, 128), b("gx", 0, 128), b("idb"))
+        mm(b("pb3", 128, 256), b("gx", 128, 256), b("idb"))
+        ts(b("f3"), b("w3"), 4095.0, OP.is_lt, 8192.0, OP.mult)
+        tt(b("cb"), b("c0"), b("cvf"), OP.max)
+        tt(b("X3", 0, 8, key="X3a"), b("bf"), vf, OP.subtract)
+        ts(b("nv"), b("iGL"), float(n0), OP.add)
+        tt(b("X3", 16, 24, key="X3b"), b("nv"), vf, OP.subtract)
+        tt(b("X3", 8, 16, key="X3c"), vf, b("dmp"), OP.subtract)
+        op("v", lambda e: e.tensor_tensor(b("g3")[0], b("pb1", 32, 56)[0], b("X3")[0], OP.mult), ["pb1", "X3a", "X3b", "X3c"], ["g3"])
+        tt(b("t3"), b("f3"), b("dvf"), OP.add)
+        tt(b("t1"), b("pb3", 0, 128), b("Mb"), OP.mult)
+        tt(b("oA"), b("g3", 8, 16), b("dmp"), OP.add)
+        cp(b("uvu"), b("oA"))
+        tt(b("q1", 0, 8), b("g3", 0, 8), b("g3", 16, 24), OP.add)
+        ts(b("Bv", 8, 16, key="Bv1"), b("oA"), float(FAR), OP.add)
+        tt(b("t2"), b("pb3", 128, 256), b("xb"), OP.mult)
+        equal("bod", ("pb3", "pb3"), "eqb")
+        ts(b("Dv", 0, 8, key="Dv0"), b("q1", 0, 8), -1.0, OP.mult)
+        tt(b("Bv", 0, 8, key="Bv0"), vf, b("q1", 0, 8), OP.add)
+        tt(b("rsp"), b("w3"), b("t3"), OP.min)
+        cp((b("C")[0].indirect(b("uvu")[0]), ["C", "uvu"]), b("ral"))
+        tt(b("An"), b("t1"), b("t2"), OP.add)
+        tt(b("hd"), b("xb"), b("abm"), OP.subtract)
+        tt(b("bd"), b("bf"), b("dmp"), OP.subtract)
+        ts(b("hc1"), b("hd"), 4.5, OP.min, -3.5, OP.max)
+        if s == 0:
+            ms(b("Dv", 8, 16, key="Dv1"), 1.0)
+        tt(b("hv"), b("hc1"), b("abm"), OP.add)
+
+        scan(b("fsm"), b("RM2"), b("pb0", 0, 128), OP.max, OP.min)
+        tt(b("Sf"), b("fsm", 15, 128, 16), b("Tt"), OP.is_lt)
+        act(b("exU"), ind(b("Sf"), bl(8)), AF.Copy)
+        expand("exS", b("Sf"), 1)
+        if t == 1:
+            tt(b("ov"), b("Sf"), b("anr0"), OP.is_lt)
+            tt(b("hF"), b("Sf"), b("gm3", 0, 8, key="ah"), OP.is_lt)
+            ts(b("nov"), b("ov"), 0.0, OP.is_equal, b("p128"), OP.mult)
+        else:
+            tt(b("hF"), b("Sf"), b("gm3", 0, 8, key="ah"), OP.is_lt)
+        to_lists_s = [("sb2", 2), ("sb3", 3)]
+        for j, (key, c) in enumerate(to_lists_s):
+            mm(b("pb1", 56 + 8 * j, 64 + 8 * j), b("exS"), b("sb", 8 * c, 8 * c + 8, key=key))
+        op("v", lambda e: e.tensor_tensor(b("q1")[0], b("pb1", 56, 72)[0], b("Dv")[0], OP.mult), ["pb1", "Dv0", "Dv1"], ["q1"])
+        if t == 1:
+            send_rank()
+        count("eqb", "hF", ("pb3", 0))
+        op("v", lambda e: e.tensor_tensor(b("vf")[0], b("q1")[0], b("Bv")[0], OP.add), ["q1", "Bv0", "Bv1"], ["vf"])
+        cp(b("vu2"), b("vf"))
+        if t == 1:
+            send_list(s)
+        cp((b("C")[0].indirect(b("vu2", 8, 16)[0]), ["C", "vu2"]), b("rsp"))
+        one = b("onesb", 0, 128, 1, 0, 1)
+        mm(b("pb2", 128, 256), b("exU"), b("GE", 128, 256, key="GE1"), True, False)
+        mm(b("pb2", 128, 256), b("exU"), b("m1c"), False, True)
+        mm(b("pb2", 0, 128), one, one, True, False)
+        mm(b("pb2", 0, 128), b("exU"), b("m1c"), False, True)
+        tt(b("h1"), b("pb3", 0, 8), b("hF"), OP.is_lt)
+        expand("exH", b("h1"), 1)
+        tt(b("C", n0, n0 + L), b("pb2", 128, 256), b("cb"), OP.max)
+        to_lists("exH", 1, ("pb1", 72), (2,))
+        tt(b("A", n0, n0 + L), b("pb2", 0, 128), b("An"), OP.mult)
+        if s == 3:
+            dma("y", "ld5", T.yc[:], b("C", 0, W)[0], ["C"], ["yc"])
+        tt(b("oA"), b("pb1", 72, 80), b("bd"), OP.mult)
+        tt(b("oA"), b("oA"), b("dmp"), OP.add)
+        cp(b("oAu"), b("oA"))
+        cp((b("A")[0].indirect(b("oAu")[0]), ["A", "oAu"]), b("hv"))
+        if s == 3:
+            dma("y", "ld6", T.ya[:], b("A", 0, W)[0], ["A"], ["ya"])
+        tt(b("nF"), b("Sf"), b("an"), OP.is_lt)
+        if t == 0:
+            tt(b("ov"), b("Sf"), b("anr0"), OP.is_lt)
+            ts(b("nov"), b("ov"), 0.0, OP.is_equal, b("p128"), OP.mult)
+            ts(b("nonr"), b("nF"), 0.0, OP.is_equal)
+            cp(b("rest"), b("nF"))
+        else:
+            tt(b("rest2"), b("rest"), b("nF"), OP.add)
+            ts(b("nonr2"), b("rest2"), 0.0, OP.is_equal)
+
+    def send_rank():
+        mm(b("pb3", 8, 16), b("tri"), b("ov"))
+        tt(b("pos"), b("pb3", 8, 16), b("nov"), OP.max)
+        expand("exP", b("pos"), 1)
+        to_lists("exP", 1, ("pb1", 80), (2,))
+
+    def send_list(s):
+        h = hops(T, topo, rank, s)
+        m = "msg%d" % s
+        cp(b("posu"), b("pb1", 80, 88))
+        cp((b(m)[0].indirect(b("posu")[0]), [m, "posu"]), b("xp"))
+        need("g", [m], [])
+        n = engines_of(topo, core, h[1])
+        rid, pid = topo.addr(h[1], core)
+        if len(h) == 3:
+            to, sem = T["rl%d" % s][:, 0:CAP], T.sem["rr%d" % s]
+        else:
+            to, sem = T["come%d" % (s // ST)][:, CAP * (s % ST):CAP * (s % ST) + CAP], T.sem["in%d" % s]
+        g.remote_dma(to, T[m][:, 0:CAP], sem, T.sem["ls%d" % s], pid, rid, emask(topo, core, h[1], n))
+
+    def arrives(s):
+        src = (rank - 1 - s % (NR - 1)) % NR
+        h = hops(T, topo, src, s)
+        wr["come%d_%d" % (s // ST, s % ST)] = ("remote", "in%d" % s, engines_of(topo, h[-2], h[-1]), {"in%d" % s: engines_of(topo, h[-2], h[-1])})
+        cnt["in%d" % s] = engines_of(topo, h[-2], h[-1])
+
+    for s in range(4):
+        arrives(s)
+
+    def round_end(s):
+        rnd = s // ST
+        cm = "come%d" % rnd
+        mm(b("pb3", 16, 24), b("tri"), b("rest2"), True, False)
+        mm(b("pb3", 16, 24), b("I128"), b("nonr2"), False, True)
+        tt(b("dM"), ind(b("A", 0, WIN), b("vu2", 0, 8)), b("xb"), OP.subtract)
+        act(b("ad"), b("dM"), AF.Abs)
+        cp(b("nrs"), b("pb3", 16, 24))
+        expand("exN", b("nrs"), 1)
+        to_lists("exN", 1, ("pb1", 88), (2,))
+        if s == 1:
+            front(2, b("tu"))
+            for c in range(4):
+                act(b("ag", 512 * c, 512 * c + 512, key="ag%d" % c), ind(b("A", 0, WIN), b("cvu", 32 * c, 32 * c + 32)), AF.Copy)
+        op("v", lambda e: e.tensor_scalar(b("msk")[0], b(cm, 0, CAP)[0], 0.5, None, OP.is_gt), [cm + "_0"], ["msk"])
+        op("v", lambda e: e.tensor_reduce(b("n0")[0], b("msk")[0], AxisListType.X, OP.add), ["msk"], ["n0"])
+        ts(b("cd"), b("n0"), -1.0, OP.mult, float(CAP), OP.add)
+        ts(b("ge"), b("pb1", 88, 96), b("n0"), OP.is_ge, b("cd"), OP.mult)
+        tt(b("idx"), b("pb1", 88, 96), b("ge"), OP.add)
+        ts(b("iu"), b("idx"), 64.0, OP.min)
+        op("v", lambda e: e.tensor_tensor(b("hx")[0], b(cm)[0].indirect(b("iu")[0]), b("ad")[0], OP.max),
+           [cm + "_0", cm + "_1", cm + "z", "iu", "ad"], ["hx"])
+        ts(b("xi"), b("hx"), 255, OP.bitwise_and)
+
+    for s in range(4):
+        t = s % ST
+        if t == 0:
+            step(s, b("tu"), b("topf"))
+            send_rank()
+            send_list(s)
+            if s == 2:
+                for k in range(16):
+                    cp(b("xrep", k, 2048, 16, key="xr"), b("xb"))
+        else:
+            step(s, b("vu2", 0, 8), b("vf", 0, 8))
+            round_end(s)
+    cp(b("xb"), b("xi"))
+    dma("y", "ld7", T.yx[:], b("xb")[0], ["xb"], ["yx"])
+    for n in sorted(cnt):
+        if cnt[n] and know["g"].get(n, 0) < cnt[n]:
+            g.wait_ge(T.sem[n], cnt[n])
+    for s in range(4):
+        g.wait_ge(T.sem["ls%d" % s], engines_of(topo, core, hops(T, topo, rank, s)[1]))

@@ -22,17 +22,18 @@ def _s(kind, **kw):
 
 _s("B", A=1680, xrep=2048, df=2048, ag=2048, ab2=2048, xb=128, xT=128, R=2048, onesb=512, zb=512, idb=128, ipb=136,
    hc=272, f16p=136, selb=8, sel2=8, bk=16, sb=32, tri=128, trib=512, kcb=408, rmask=384, Di=128, I128=128, GN=640, GE=256,
-   PS=256, m1c=128, bb=143, bs=1664, EE=128, Tb=1664, h8=128, Fm=128, cod=128, codE=128, codO=128, bod=128, bodE=128, bodO=128,
+   m1c=128, bb=143, bs=1664, EE=128, Tb=1664, h8=128, Fm=128, cod=128, codE=128, codO=128, bod=128, bodE=128, bodO=128,
    eqa=1024, eqb=1024, ex=256, ex2=256, oh=384, gx=256, gm=384, exS=128, exU=128, exH=128, exP=128, exN=128, absM=128, Mb=128,
-   An=128, hv=128, hF=8, ov=8, nov=8, rest=8, rest2=8, nonr=8, nonr2=8, one8=8, nF=8, dA=128)
-_s("F", C=3840, idf=136, zf=272, RM=272, RM2=128, kcf=408, kcg=408, kpat=384, iGL=8, dmp=8, lim=8, lim1=8, thf=128, topf=8,
-   r=128, y=128, cvf=128, dvf=128, m1=272, m2=272, cand=272, k0s=136, k031=8, abm=128, sm=128, ym=128, xs=128, xp=128, dM=128,
-   hm=8, he=8, nn=8, T0=8, Tt=8, act0=8, act1=8, an=8, ah0=8, gk=24, kk=24, k1=8, k2=8, wal=128, ral=128, w3=128, f3=128, t3=128,
-   rsp=128, c0=128, cb=128, t1=128, t2=128, am2=16, X3=24, g3=24, gm3=32, Dv=16, Bv=16, q1=16, vf=16, bf=8, fsm=128, Sf=8, anr0=8, nrm=8, h1=8,
-   oA=8, pos=8, nrs=8, hd=128, hc1=128, ge=8, idx=8, msk=32, n0=1, cd=1, ad=128, mE=1, mO=1, nv=8, bd=8, p128=1)
-_s("I", KI=1024, tp=8, thi=128, ci=128, rmi=384, pin=8, pr=8, m16=8, cio=13, bt=143, m1e=16, dec=16, eb=8, kb=8, m2e=16,
-   dec2=16, kq=8, hx=128, xi=128, iv=8, ip=8)
+   An=128, hv=128, hF=8, ov=8, nov=8, rest=8, rest2=8, nonr=8, nonr2=8, one8=8, nF=8)
+_s("F", CW=FAR + 1680, idf=136, zf=272, RM=272, RM2=128, kcf=408, kcg=408, kpat=384, iGL=8, dmp=8, dmp16=8, lim=8, lim1=8, thf=128, topf=16,
+   r=128, y=128, cvf=128, dvf=128, m1=272, m2=272, cand=272, k0s=136, abm=128, sm=128, ym=128, xs=128, xp=128, dM=128,
+   hm=8, he=8, nn=8, T0=8, Tt=8, act0=8, an=8, ah0=8, k1=8, k2=8, wal=128, ral=128, w3=128, f3=128, t3=128, v16=8, nv=8,
+   rsp=128, c0=128, cb=128, t1=128, t2=128, X3=24, g3=24, gm3=32, Dv=16, q1=16, vf=16, fsm=128, Sf=8, anr0=8, nrm=8, h1=8,
+   oA=8, pos=8, nrs=8, hd=128, hc1=128, ge=8, idx=8, msk=32, n0=1, cd=1, ad=128, mE=1, mO=1, bd=8, p128=1)
+_s("I", KI=1024, tp=8, thi=128, ci=128, rmi=384, pin=8, pr=8, m16=8, cio=13, bt=143, m1e=16, dec=16, eb=8, kk=24, m2e=16,
+   dec2=16, kq=8, hx=128, xi=128, iv=8)
 _s("U", bl=128, tu=8, cvu=128, dvu=128, bu=8, qu=8, uvu=8, vu2=16, oAu=8, posu=8, iu=8)
+SLOT["C"] = ("arF", SLOT["CW"][1] + FAR, 1680)
 
 SCRATCH = {"arF": ("sbuf", [128, SIZE["F"]], "float32"), "arB": ("sbuf", [128, SIZE["B"]], "bfloat16"),
            "arI": ("sbuf", [128, SIZE["I"]], "int32"), "arU": ("sbuf", [128, SIZE["U"]], "uint16")}
@@ -146,16 +147,13 @@ def rank_program(g, core, T, topo):
         else:
             buf, o, w = name, 0, SCRATCH[name][1][1]
         c1 = w if c1 is None else c1
-        return (T[buf][p0:p1, o + c0:o + c1:st] if st != 1 else T[buf][p0:p1, o + c0:o + c1], [key or name])
+        return (T[buf][p0:p1, o + c0:o + c1:st] if st != 1 else T[buf][p0:p1, o + c0:o + c1], key if isinstance(key, list) else [key or name])
 
     def ind(win, off):
         return (win[0].indirect(off[0]), win[1] + off[1])
 
     def ks(*refs):
         return [k for r in refs if isinstance(r, tuple) for k in r[1]]
-
-    def split_out(o):
-        return (o[1][1:] if len(o[1]) > 1 else []), o[1][:1]
 
     def ap(x):
         return x[0] if isinstance(x, tuple) else x
@@ -170,8 +168,10 @@ def rank_program(g, core, T, topo):
             op("v", lambda e: e.tensor_scalar(o[0], a[0], ap(s1), ap(s2), f0, f1), ks(a, s1, s2), ks(o))
 
     def cp(o, a):
-        r, w = split_out(o)
-        op("v", lambda e: e.tensor_copy(o[0], a[0]), ks(a) + r, w)
+        op("v", lambda e: e.tensor_copy(o[0], a[0]), ks(a), ks(o))
+
+    def scatter(win, off, a):
+        op("v", lambda e: e.tensor_copy(win[0].indirect(off[0]), a[0]), ks(a, off), ks(win))
 
     def ms(o, v):
         op("v", lambda e: e.memset(o[0], v), [], ks(o))
@@ -195,49 +195,62 @@ def rank_program(g, core, T, topo):
         op("g", lambda e: e.affine_select(o[0], a[0], pat, f, fill, base, cm), ks(a), ks(o))
 
     bl = lambda n, c0=0: b("bl", c0, c0 + n)
+    one = b("onesb", 0, 128, 1, 0, 1)
 
-    ms(b("A", V0, W), 0.0)
-    ms(b("A", W, WIN), 4096.0)
     dma("y", "ld0", b("tp")[0], T.tops[:], [], ["tp"])
     dma("y", "ld1", b("xb")[0], T.x0[:], [], ["xb"])
     dma("y", "ld2", b("KI")[0], T.kids[:], [], ["KI"])
-    dma("y", "ld3", b("A", 0, V0)[0], T.a0[:], [], ["A"])
     dma("s", "ld4", b("thi", 0, 128, 1, 0, 8)[0], T.th[:], [], ["thi"])
-
+    ms(b("A", V0, W), 0.0)
+    ms(b("A", W, WIN), 4096.0)
+    dma("y", "ld3", b("A", 0, V0)[0], T.a0[:], [], ["A"])
     ms(b("onesb"), 1.0)
     ms(b("zf"), 0.0)
+    ms(b("zb"), 0.0)
+    for k in range(2):
+        ms(b("come%d" % k, 64, 80, key="come%dz" % k), 0.0)
+    for k in range(4):
+        ms(b("msg%d" % k, 0, CAP), 0.0)
+    io(b("cio"), [[128, 13]], 0, 1)
     io(b("ci"), [[1, 128]], 0, 0)
-    cp(b("bl"), b("ci"))
-    cp(b("tu"), b("tp"))
-    cp(b("topf"), b("tp"))
-    for k in range(16):
-        cp(b("xrep", k, 2048, 16, key="xr"), b("xb"))
-    ms(b("C", V0, WIN), 4095.0)
     asel(b("idb"), b("onesb", 0, 128), [[-1, 128]], OP.is_equal, 0.0, 0, 1)
+    asel(b("EE", p1=16), b("onesb", 0, 128, 1, 0, 16), [[0, 8], [-1, 16]], OP.is_equal, 0.0, 0, 1)
     asel(b("ipb"), b("onesb", 0, 136), [[-16, 8], [-1, 17]], OP.is_equal, 0.0, 1, 1)
-    io(b("kcf", 0, 136, key="kcf0"), [[0, 8], [128, 17]], -64, 0, True)
-    io(b("kcf", 136, 272, key="kcf1"), [[0, 8], [128, 17]], -128, 0, True)
-    io(b("kcf", 272, 408, key="kcf2"), [[0, 8], [1, 17]], -1, 0, True)
-    op("g", lambda e: e.affine_select(b("kcg")[0], b("kcf")[0], [[0, 24], [1, 17]], OP.not_equal, BIG, 0, 0), ["kcf0", "kcf1", "kcf2"], ["kcg"])
+    io(b("kcf", 0, 136, key="kcf0"), [[0, 8], [128, 17]], 64, 0, True)
+    io(b("kcf", 136, 272, key="kcf1"), [[0, 8], [128, 17]], 0, 0, True)
+    io(b("kcf", 272, 408, key="kcf2"), [[0, 8], [1, 17]], 0, 0, True)
+    asel(b("kcg"), b("kcf", key=["kcf0", "kcf1", "kcf2"]), [[0, 24], [1, 17]], OP.not_equal, BIG, 0, 0)
     asel(b("sel2"), b("onesb", 0, 8), [[-16, 8]], OP.is_ge, 0.0, 0, 1)
     asel(b("selb"), b("sel2"), [[16, 8]], OP.is_ge, 0.0, 15, -1)
-    asel(b("RM"), b("zf"), [[0, 16], [1, 17]], OP.not_equal, BIG, 0, 0)
-    io(b("rmi"), [[0, 24], [-1, 16]], 16, 1)
-    io(b("cio"), [[128, 13]], 0, 1)
-    ms(b("R"), -1.0)
-    asel(b("R"), b("R"), [[-1, 128], [0, 16]], OP.is_equal, 0.0, 0, 1)
     io(b("pin"), [[0, 8]], 0, 1)
     io(b("m16"), [[16, 8]], 0, 0)
-    io(b("kpat"), [[0, 24], [1, 16]], -31, 0, True)
-    ms(b("zb"), 0.0)
-    asel(b("EE", p1=16), b("onesb", 0, 128, 1, 0, 16), [[0, 8], [-1, 16]], OP.is_equal, 0.0, 0, 1)
+    asel(b("RM"), b("zf"), [[0, 16], [1, 17]], OP.not_equal, BIG, 0, 0)
+    io(b("rmi"), [[0, 24], [-1, 16]], 16, 1)
     asel(b("trib"), b("zb"), [[0, 4], [1, 128]], OP.is_gt, -32.0, 0, -1)
+    io(b("kpat"), [[0, 24], [1, 16]], 1, 0, True)
     asel(b("tri"), b("onesb", 0, 128), [[1, 128]], OP.is_gt, 0.0, 0, -1)
     asel(b("RM2"), b("zf", 0, 128), [[0, 8], [1, 16]], OP.not_equal, BIG, 0, 0)
-    for k in range(4):
-        io(b("msg%d" % k, 0, CAP), [[0, CAP]], 0, 0, True)
-    for k in range(2):
-        io(b("come%d" % k, 64, 80, key="come%dz" % k), [[0, 16]], 0, 0, True)
+
+    ms(b("C", V0, WIN), 4095.0)
+    for k in range(11):
+        ts(b("bt", 13 * k, 13 * k + 13, key="bt"), b("cio"), k, OP.logical_shift_right, 1, OP.bitwise_and)
+    ts(b("bb"), b("bt"), 2.0, OP.mult, -1.0, OP.add)
+    cp(b("bl"), b("ci"))
+    cp(b("tu"), b("tp"))
+    cp(b("topf", 0, 8, key="topf"), b("tp"))
+    for k in range(16):
+        cp(b("xrep", k, 2048, 16, key="xr"), b("xb"))
+    for k in range(16):
+        act(b("R", k, 2048, 16, key="R"), b("idb"), AF.Copy, 0.0, -1.0)
+    for q in range(13):
+        mm(b("pb%d" % (4 + q // 4), 128 * (q % 4), 128 * (q % 4) + 128, 1, 0, 11), b("bb", q, 143, 13), b("idb"))
+    for h in range(4):
+        n = 512 if h < 3 else 128
+        act(b("bs", 512 * h, 512 * h + n, 1, 0, 11, key="bs%d" % h), b("pb%d" % (4 + h), 0, n, 1, 0, 11), AF.Copy)
+    for h in range(4):
+        n = 512 if h < 3 else 128
+        mm(b("pb%d" % (4 + h), 0, n), b("EE", p1=11), b("bs", 512 * h, 512 * h + n, 1, 0, 11, key="bs%d" % h))
+        act(b("Tb", 512 * h, 512 * h + n), b("pb%d" % (4 + h), 0, n), AF.Copy)
 
     def consts_a():
         cp(b("idf"), b("ipb"))
@@ -245,44 +258,34 @@ def rank_program(g, core, T, topo):
         cp(b("hc", 136, 272, key="hc1"), b("ipb"))
         ts(b("f16p"), b("ipb"), 16.0, OP.mult)
         cp(b("kcb"), b("kcg"))
-        ts(b("bk", 0, 8, key="bk0"), b("selb"), 2048.0, OP.mult)
-        ts(b("bk", 8, 16, key="bk1"), b("selb"), 2048.0, OP.mult)
+        ts(b("bk", 0, 8, key="bk0"), b("selb"), 4096.0, OP.mult)
+        ts(b("bk", 8, 16, key="bk1"), b("selb"), 4096.0, OP.mult)
 
     def consts_b():
-        for j, m in enumerate((-1.0, -16.0, 1.0, -2048.0)):
+        ts(b("iv"), b("pin"), 4, OP.logical_shift_right, 1, OP.bitwise_and)
+        for j, m in enumerate((-1.0, -16.0, 1.0, float(FAR))):
             ts(b("sb", 8 * j, 8 * j + 8, key="sb%d" % j), b("selb"), m, OP.mult)
         ts(b("rmi"), b("rmi"), 15, OP.bitwise_and)
+        cp(b("mO"), b("iv", 0, 1))
+        ts(b("mE"), b("iv", 0, 1), -1.0, OP.mult, 1.0, OP.add)
         ts(b("rmask"), b("rmi"), 0.0, OP.is_equal)
+        ts(b("pr"), b("pin"), 15, OP.bitwise_and)
+        ms(b("one8"), 1.0)
+        ms(b("Dv", 8, 16, key="Dv1"), 1.0)
+        tt(b("iGL"), b("pr"), b("m16"), OP.add)
+        ts(b("p128"), b("pin", 0, 1), 128.0, OP.add)
+        ts(b("dmp"), b("iGL"), float(DUMP), OP.add)
+        ts(b("dmp16"), b("iGL"), float(DUMP - 1600), OP.add)
 
     def consts_c():
-        ms(b("one8"), 1.0)
         cp(b("thf", 0, 128, 1, 0, 8), b("thi", 0, 128, 1, 0, 8))
         mm(b("pb3", 0, 8), b("thf", 0, 128, 1, 0, 8), b("idf", 1, 9, 1, 0, 8))
         cp(b("lim"), b("pb3", 0, 8))
         ts(b("lim1"), b("lim"), 1.0, OP.add)
-        ts(b("pr"), b("pin"), 15, OP.bitwise_and)
-        tt(b("iGL"), b("pr"), b("m16"), OP.add)
-        ts(b("dmp"), b("iGL"), float(DUMP), OP.add)
-        for k in range(11):
-            ts(b("bt", 13 * k, 13 * k + 13, key="bt"), b("cio"), k, OP.logical_shift_right, 1, OP.bitwise_and)
-        ts(b("bb"), b("bt"), 2.0, OP.mult, -1.0, OP.add)
-        for q in range(13):
-            mm(b("pb%d" % (4 + q // 4), 128 * (q % 4), 128 * (q % 4) + 128, 1, 0, 11), b("bb", q, 143, 13), b("idb"))
-        for h in range(4):
-            n = 512 if h < 3 else 128
-            act(b("bs", 512 * h, 512 * h + n, 1, 0, 11, key="bs%d" % h), b("pb%d" % (4 + h), 0, n, 1, 0, 11), AF.Copy)
-        for h in range(4):
-            n = 512 if h < 3 else 128
-            mm(b("pb%d" % (4 + h), 0, n), b("EE", p1=11), b("bs", 512 * h, 512 * h + n, 1, 0, 11, key="bs%d" % h))
-            act(b("Tb", 512 * h, 512 * h + n), b("pb%d" % (4 + h), 0, n), AF.Copy)
-        ts(b("iv"), b("pin"), 4, OP.logical_shift_right, 1, OP.bitwise_and)
-        cp(b("mO"), b("iv", 0, 1))
-        ts(b("mE"), b("iv", 0, 1), -1.0, OP.mult, 1.0, OP.add)
 
     def consts_d():
         tt(b("Di"), b("idb"), b("ci"), OP.mult)
         ts(b("I128"), b("idb"), 128.0, OP.mult)
-        ts(b("p128"), b("pin", 0, 1), 128.0, OP.add)
         ts(b("GN", 0, 128, key="GNa"), b("idb"), 8192.0, OP.mult)
         for s in range(4):
             ts(b("GN", 128 + 128 * s, 256 + 128 * s, key="GN%d" % s), b("idb"), float(128 * (s - 56)), OP.mult)
@@ -298,27 +301,23 @@ def rank_program(g, core, T, topo):
         mm(b("pb3", 0, 128), b("xb"), b("idb"))
         act(b("xT"), b("pb3", 0, 128), AF.Copy)
 
-    def preload_x():
-        for c in range(4):
+    def preload_x(cs):
+        for c in cs:
             mm(b("pb%d" % (4 + c)), b("xT"), b("R", 512 * c, 512 * c + 512), True, False)
 
-    def codes(u, d):
-        act(b(d), ind(b("Tb", 0, WIN), u), AF.Copy)
-        act(b(d + "E"), b(d), AF.Copy, 0.0, b("mE"))
-        act(b(d + "O"), b(d), AF.Copy, 0.0, b("mO"))
+    def codes_masked(d):
+        ts(b(d + "E"), b(d), b("mE"), OP.mult)
+        ts(b(d + "O"), b(d), b("mO"), OP.mult)
 
-    def equal(d, banks, out):
-        for h in range(2):
-            bank = banks[h]
-            mm(b(bank), b("idb"), b("trib"), True, False)
-            for j in range(4):
-                w = 4 * h + j
-                p = w // 2 * 32
-                if j == 2:
-                    need("t", [bank], [])
-                mm(b(bank, 128 * j, 128 * j + 128), b(d, 0, 128, 1, p, p + 32), b(d + ("O" if w % 2 else "E"), 0, 128, 1, p, p + 32),
-                   False, j == 3)
-            act(b(out, 512 * h, 512 * h + 512, key=out + str(h)), b(bank), AF.Relu, -10.0)
+    def equal(d, bank, h):
+        mm(b(bank), b("idb"), b("trib"), True, False)
+        for j in range(4):
+            w = 4 * h + j
+            p = w // 2 * 32
+            if j == 2:
+                need("t", [bank], [])
+            mm(b(bank, 128 * j, 128 * j + 128), b(d, 0, 128, 1, p, p + 32), b(d + ("O" if w % 2 else "E"), 0, 128, 1, p, p + 32),
+               False, j == 3)
 
     def count(eq, mask, o):
         for w in range(8):
@@ -331,216 +330,243 @@ def rank_program(g, core, T, topo):
     def expand(ex, src, n):
         tt(b(ex, 0, 128 * n), ind(src, bl(8 * n)), b("rmask", 0, 128 * n), OP.mult)
 
+    def front_v(s, vu):
+        ts(b("cvu"), ind(b("KI") if s == 0 else b("C", 0, WIN), vu), float(E1), OP.min)
+
     def front(s, vu):
-        if s == 0:
-            ts(b("cvu"), ind(b("KI"), vu), float(E1), OP.min)
-            cp(b("C", 0, V0), b("KI"))
-        else:
-            ts(b("cvu"), ind(b("C", 0, WIN), vu), float(E1), OP.min)
         act(b("r"), ind(b("C", 0, WIN), vu), AF.Relu, float(E1), -1.0)
         act(b("y"), b("r"), AF.Identity, MAGIC, 1.0 / 127.95)
         act(b("h8"), b("y"), AF.Identity, -8 * MAGIC, 8.0)
         act(b("Fm"), b("r"), AF.Sign)
-        if s == 0:
-            consts_a()
-        one = b("onesb", 0, 128, 1, 0, 1)
         mm(b("pb0", 272, 408), one, b("kcb", 272, 408, 1, 0, 1), True, False)
         mm(b("pb0", 272, 408), b("Fm"), b("f16p"), False, True)
         mm(b("pb0", 0, 272), one, b("kcb", 0, 272, 1, 0, 1), True, False)
         mm(b("pb0", 0, 136), b("r"), b("idf"), False, False)
-        op("t", lambda e: e.matmul(b("pb0", 0, 272)[0], b("h8")[0], b("hc")[0], False, False), ["h8", "hc0", "hc1"], ["pb0"])
+        mm(b("pb0", 0, 272), b("h8"), b("hc", key=["hc0", "hc1"]), False, False)
 
-    act_name = {0: "act0", 1: "act1", 2: "act0", 3: "act1"}
-
-    def step(s, vu, vf):
+    def step(s, vu, tv):
         t = s % ST
-        rnd = s // ST
         n0 = V0 + L * s
+        vf = b(tv, 0, 8)
+        if s == 0:
+            front_v(0, vu)
+            cp(b("C", 0, V0), b("KI"))
+            consts_a()
         if s != 2:
             front(s, vu)
         if s == 0:
-            x_forms(b("xb"))
             turn_x()
-        if t == 1:
-            codes(vu, "cod")
-        if t == 1:
-            preload_x()
+        if s != 2:
+            preload_x((0, 1, 2, 3))
         for j, (l0, n) in enumerate(PIECES):
             c0, c1 = 16 * l0, 16 * (l0 + n)
+            dj = b("df", c0, c1, key="df%d" % j)
             if s == 2:
-                tt(b("df", c0, c1, key="df%d" % j), ind(b("xi"), bl(n, l0)), b("ag", c0, c1, key="ag%d" % (l0 // 32)), OP.subtract)
+                tt(dj, ind(b("xi"), bl(n, l0)), b("ag", c0, c1, key="ag%d" % (l0 // 32)), OP.subtract)
                 if j == 0:
                     cp(b("xb"), b("xi"))
-                    turn_x()
-                    preload_x()
             else:
-                op("v", lambda e: e.tensor_tensor(b("df", c0, c1)[0], ind(b("A", 0, WIN), b("cvu", l0, l0 + n))[0], b("xrep", c0, c1)[0], OP.subtract),
-                   ["A", "cvu", "xr"], ["df%d" % j])
-            act(b("df", c0, c1, key="df%d" % j), b("df", c0, c1, key="df%d" % j), AF.Abs)
+                tt(dj, ind(b("A", 0, WIN), b("cvu", l0, l0 + n)), b("xrep", c0, c1, key="xr"), OP.subtract)
+            act(dj, dj, AF.Abs)
+            if s == 2 and j == 0:
+                turn_x()
+            if j == 0 and s != 2:
+                act(b("cvf"), ind(b("C", 0, WIN), vu), AF.Copy)
         for l0, l1, js in ((0, 96, (0, 1, 2)), (96, 128, (3, 4))):
             for k in range(16):
-                op("t", lambda e: e.matmul(b("pb0", 1 + k, 272, 17, l0, l1)[0], b("df", 16 * l0 + k, 16 * l1, 16)[0], b("bk")[0], False, k == 15),
-                   ["df%d" % j for j in js] + ["bk0", "bk1"], ["pb0"])
+                mm(b("pb0", 1 + k, 272, 17, l0, l1), b("df", 16 * l0 + k, 16 * l1, 16, key=["df%d" % j for j in js]),
+                   b("bk", key=["bk0", "bk1"]), False, k == 15)
+        if s != 2:
+            act(b("cod"), ind(b("Tb", 0, WIN), vu), AF.Copy)
+        if t == 1:
+            tt(b("nF"), b("Sf"), b("an"), OP.is_lt)
+            tt(b("ov"), b("Sf"), b("anr0"), OP.is_lt)
+            ts(b("nonr"), b("nF"), 0.0, OP.is_equal)
+            ts(b("nov"), b("ov"), 0.0, OP.is_equal, b("p128"), OP.mult)
+            cp(b("rest"), b("nF"))
+            mm(b("pb1", 96, 104), b("tri"), b("ov"))
         if s == 0:
             consts_b()
-        if s == 2:
-            x_forms(b("xi"))
+        if s != 2:
+            codes_masked("cod")
+        ts(b("nv"), b("iGL"), float(n0), OP.add)
+        if s in (0, 2):
+            x_forms(b("xb"))
+        tt(b("X3", 8, 16, key="X3c"), vf, b("dmp"), OP.subtract)
+        tt(b("X3", 16, 24, key="X3b"), b("nv"), vf, OP.subtract)
+        ts(b("v16"), vf, -1600.0, OP.add)
         scan(b("m1"), b("RM"), b("pb0", 0, 272), OP.max, OP.min)
         cp(b("m1e"), b("m1", 16, 272, 17))
         ts(b("dec"), b("m1e"), 127, OP.bitwise_and)
         expand("ex", b("dec"), 2)
-        scan(b("k0s"), b("RM", 0, 136), b("pb0", 272, 408), OP.max, OP.min)
+        if s == 2:
+            preload_x((0, 1))
+            for k in range(8):
+                act(b("xrep", k, 2048, 16, key="xr"), b("xb"), AF.Copy)
+        else:
+            equal("cod", "pb2", 0)
+            act(b("eqa", 0, 512, key="eqa0"), b("pb2"), AF.Relu, -10.0)
         to_b = b("pb1", 0, 8)
         mm(to_b, b("ex", 0, 128), b("sb", 0, 8, key="sb0"), True, False)
         mm(to_b, b("ex", 128, 256), b("sb", 8, 16, key="sb1"), False, True)
+        if s == 2:
+            preload_x((2, 3))
+        else:
+            equal("cod", "pb3", 1)
+            act(b("eqa", 512, 1024, key="eqa1"), b("pb3"), AF.Relu, -10.0)
+        if t == 1:
+            send_rank()
+        scan(b("k0s"), b("RM", 0, 136), b("pb0", 272, 408), OP.max, OP.min)
         ts(b("bu"), to_b, 1600.0, OP.add)
         ts(b("dvu"), ind(b("C", 0, WIN), b("bu")), float(E1), OP.min)
-        ts(b("bf"), to_b, 1600.0, OP.add)
-        act(b("cvf"), ind(b("C", 0, WIN), vu), AF.Copy)
+        if s != 2:
+            count("eqa", "nonr" if t == 1 else "one8", ("pb1", 16))
         act(b("abm"), ind(b("A", 0, WIN), b("bu")), AF.Identity, -0.5)
-        if s == 0:
-            consts_c()
-            codes(b("tu"), "cod")
-            preload_x()
-        if t == 1 or s == 0:
-            equal("cod", ("pb2", "pb3"), "eqa")
-        op("v", lambda e: e.tensor_tensor(b("cand", 1, 272)[0], b("m1", 0, 271)[0], b("pb0", 1, 272)[0], OP.max), ["m1", "pb0"], ["cand"])
-        op("v", lambda e: e.tensor_tensor_scan(b("m2", 1, 272)[0], b("RM", 1, 272)[0], b("cand", 1, 272)[0], BIG, OP.max, OP.min), ["RM", "cand"], ["m2"])
+        tt(b("cand", 1, 272), b("m1", 0, 271), b("pb0", 1, 272), OP.max)
+        tt(b("X3", 0, 8, key="X3a"), to_b, b("v16"), OP.subtract)
+        scan(b("m2", 1, 272), b("RM", 1, 272), b("cand", 1, 272), OP.max, OP.min)
+        tt(b("bd"), to_b, b("dmp16"), OP.subtract)
         cp(b("m2e"), b("m2", 16, 272, 17))
+        ts(b("eb"), b("m1e", 0, 8), 12, OP.logical_shift_right)
         ts(b("dec2"), b("m2e"), 127, OP.bitwise_and)
+        ts(b("kk", 0, 8, key="kk0"), b("m1e", 0, 8), 7, OP.logical_shift_right, 31, OP.bitwise_and)
         expand("ex2", b("dec2"), 2)
         to_q = b("pb1", 8, 16)
         mm(to_q, b("ex2", 0, 128), b("sb", 0, 8, key="sb0"), True, False)
         mm(to_q, b("ex2", 128, 256), b("sb", 8, 16, key="sb1"), False, True)
-        ts(b("eb"), b("m1e", 0, 8), 11, OP.logical_shift_right)
-        ts(b("kb"), b("m1e", 0, 8), 7, OP.logical_shift_right, 15, OP.bitwise_and)
-        ts(b("kq"), b("m2e", 0, 8), 7, OP.logical_shift_right, 15, OP.bitwise_and)
+        ts(b("kq"), b("m2e", 0, 8), 7, OP.logical_shift_right, 31, OP.bitwise_and)
+        ts(b("nrm"), b("k0s", 16, 136, 17), 16.0, OP.is_gt)
         ts(b("qu"), to_q, 1600.0, OP.add)
         tt(b("sm"), ind(b("A", 0, WIN), b("qu")), b("abm"), OP.add)
+        if s == 0:
+            consts_c()
         ts(b("ym"), b("sm"), 0.5, OP.mult, MAGIC, OP.add)
         tt(b("dM"), b("xs"), b("ym"), OP.subtract)
+
         def gather(c):
             act(b("ag", 512 * c, 512 * c + 512, key="ag%d" % c), ind(b("A", 0, WIN), b("dvu", 32 * c, 32 * c + 32)), AF.Copy)
+
+        def less_x(c):
             mm(b("pb%d" % (4 + c)), b("idb"), b("ag", 512 * c, 512 * c + 512, key="ag%d" % c), False, True)
 
         def away(c):
             act(b("ab2", 512 * c, 512 * c + 512, key="ab2%d" % c), b("pb%d" % (4 + c)), AF.Abs)
 
         gather(0)
+        less_x(0)
+        act(b("bod"), ind(b("Tb", 0, WIN), b("bu")), AF.Copy)
         gather(1)
-        away(0)
-        if t == 1 or s == 0:
-            count("eqa", "nonr" if t == 1 else "one8", ("pb1", 16))
-        gather(2)
+        less_x(1)
         act(b("absM"), b("dM"), AF.Abs)
-        act(b("Mb"), b("ym"), AF.Identity, -MAGIC)
         mm(b("pb1", 24, 32), b("absM"), b("selb"))
-        act(b("dvf"), ind(b("C", 0, WIN), b("bu")), AF.Copy)
+        codes_masked("bod")
+        equal("bod", "pb3", 0)
+        away(0)
+        gather(2)
+        less_x(2)
+        act(b("Mb"), b("ym"), AF.Identity, -MAGIC)
         away(1)
         gather(3)
+        act(b("dvf"), ind(b("C", 0, WIN), b("bu")), AF.Copy)
         away(2)
 
-        ac = act_name[s]
-        if s == 0 or t == 1:
-            tt(b(ac), b("pb1", 16, 24), b("one8" if s == 0 else "nonr"), OP.is_lt)
+        tt(b("hd"), b("xb"), b("abm"), OP.subtract)
+        ts(b("hc1"), b("hd"), 4.5, OP.min, -3.5, OP.max)
+        tt(b("hv"), b("hc1"), b("abm"), OP.add)
+        ac = b("gm3", 8, 16, key="ac")
+        if s == 2:
+            cp(ac, b("act0"))
+        else:
+            tt(ac, b("pb1", 16, 24), b("one8" if s == 0 else "nonr"), OP.is_lt)
         em = b("pb1", 24, 32)
+        ah, am = b("gm3", 0, 8, key="ah"), b("gm3", 16, 24, key="am")
         tt(b("hm"), em, b("eb"), OP.min)
         tt(b("he"), em, b("eb"), OP.is_ge)
-        ts(b("k031"), b("k0s", 16, 136, 17), -31.0, OP.add)
         tt(b("nn"), b("lim"), b("hm"), OP.is_lt)
         tt(b("T0"), b("lim1"), b("hm"), OP.min)
-        tt(b("an"), b("nn"), b(ac), OP.mult)
-        tt(b("Tt"), b("T0"), b(ac), OP.mult)
-        tt(b("ah0"), b(ac), b("an"), OP.subtract)
-        ts(b("nrm"), b("k031"), -15.0, OP.is_ge)
-        tt(b("gm3", 0, 8, key="ah"), b("ah0"), b("he"), OP.mult)
-        ts(b("kk", 0, 8, key="kk0"), b("kb"), -31.0, OP.add)
+        tt(b("an"), b("nn"), ac, OP.mult)
+        tt(b("Tt"), b("T0"), ac, OP.mult)
+        tt(b("ah0"), ac, b("an"), OP.subtract)
+        tt(b("k2"), b("an"), b("k0s", 16, 136, 17), OP.mult)
+        tt(ah, b("ah0"), b("he"), OP.mult)
         tt(b("anr0"), b("an"), b("nrm"), OP.mult)
-        tt(b("gm3", 16, 24, key="am"), b("ah0"), b("gm3", 0, 8, key="ah"), OP.subtract)
-        ts(b("nv"), b("kq"), -31.0, OP.add)
-        tt(b("k2"), b("an"), b("k031"), OP.mult)
-        tt(b("k1"), b("gm3", 16, 24, key="am"), b("kk", 0, 8, key="kk0"), OP.mult)
-        tt(b("kk", 16, 24, key="kk2"), b("gm3", 16, 24, key="am"), b("nv"), OP.mult)
+        tt(am, b("ah0"), ah, OP.subtract)
+        if s == 0:
+            cp(b("act0"), ac)
+        tt(b("k1"), am, b("kk", 0, 8, key="kk0"), OP.mult)
+        tt(b("kk", 16, 24, key="kk2"), am, b("kq"), OP.mult)
         tt(b("kk", 8, 16, key="kk1"), b("k1"), b("k2"), OP.add)
         tt(b("gm3", 24, 32, key="ax"), b("an"), b("anr0"), OP.subtract)
-        cp(b("gm3", 8, 16, key="ac"), b(ac))
-        op("v", lambda e: e.tensor_tensor(b("oh")[0], ind(b("kk"), bl(24))[0], b("kpat")[0], OP.is_equal), ["kk0", "kk1", "kk2", "bl", "kpat"], ["oh"])
+        tt(b("oh"), ind(b("kk", key=["kk0", "kk1", "kk2"]), bl(24)), b("kpat"), OP.is_equal)
         if s == 0:
             consts_d()
         ohb, ohn, ohe = b("oh", 0, 128), b("oh", 128, 256), b("oh", 256, 384)
         i8 = b("GN", 0, 128, key="GNa")
+        mm(b("pb2", 256, 384), ohb, i8)
         mm(b("pb2", 0, 128), ohn, i8, True, False)
         mm(b("pb2", 0, 128), ohe, i8, False, True)
         mm(b("pb2", 128, 256), ohn, b("GN", 128 + 128 * s, 256 + 128 * s, key="GN%d" % s), True, False)
         mm(b("pb2", 128, 256), ohn, b("Di"), False, False)
         mm(b("pb2", 128, 256), ohe, b("GE", 0, 128, key="GE0"), False, False)
         mm(b("pb2", 128, 256), ohe, b("m1c"), False, True)
-        mm(b("pb2", 256, 384), ohb, i8)
-        op("v", lambda e: e.tensor_tensor(b("gm")[0], ind(b("gm3", 0, 24), bl(24))[0], b("rmask")[0], OP.mult), ["ah", "am", "ac", "bl", "rmask"], ["gm"])
+        tt(b("gm"), ind(b("gm3", 0, 24, key=["ah", "ac", "am"]), bl(24)), b("rmask"), OP.mult)
         to_lists("gm", 3, ("pb1", 32), (2, 2, 2))
+        less_x(3)
+        act(b("gx"), ind(b("gm3", 16, 32, key=["am", "ax"]), bl(16)), AF.Copy)
         away(3)
-        op("s", lambda e: e.activation(b("gx")[0], ind(b("gm3", 16, 32), bl(16))[0], AF.Copy, bias=0.0, scale=1.0), ["am", "ax", "bl"], ["gx"])
+        mm(b("pb5", 0, 128), b("gx", 0, 128), b("idb"))
+        mm(b("pb5", 128, 256), b("gx", 128, 256), b("idb"))
+        equal("bod", "pb4", 1)
         for l0, l1, cs in ((0, 96, (0, 1, 2)), (96, 128, (3,))):
             for k in range(16):
-                op("t", lambda e: e.matmul(b("pb0", k, 128, 16, l0, l1)[0], b("ab2", 16 * l0 + k, 16 * l1, 16)[0], b("selb")[0], True, True),
-                   ["ab2%d" % c for c in cs] + ["selb"], ["pb0"])
-        codes(b("bu"), "bod")
-        tt(b("wal"), b("cvf"), b("pb2", 0, 128), OP.max)
-        tt(b("ral"), b("wal"), b("pb2", 128, 256), OP.add)
+                mm(b("pb0", k, 128, 16, l0, l1), b("ab2", 16 * l0 + k, 16 * l1, 16, key=["ab2%d" % c for c in cs]), b("selb"))
         tt(b("w3"), b("cvf"), b("pb2", 256, 384), OP.max)
-        ts(b("c0"), b("pb2", 0, 128), 0.0, OP.is_equal, 4095.0, OP.mult)
-        mm(b("pb3", 0, 128), b("gx", 0, 128), b("idb"))
-        mm(b("pb3", 128, 256), b("gx", 128, 256), b("idb"))
-        ts(b("f3"), b("w3"), 4095.0, OP.is_lt, 8192.0, OP.mult)
-        tt(b("cb"), b("c0"), b("cvf"), OP.max)
-        tt(b("X3", 0, 8, key="X3a"), b("bf"), vf, OP.subtract)
-        ts(b("nv"), b("iGL"), float(n0), OP.add)
-        tt(b("X3", 16, 24, key="X3b"), b("nv"), vf, OP.subtract)
-        tt(b("X3", 8, 16, key="X3c"), vf, b("dmp"), OP.subtract)
-        op("v", lambda e: e.tensor_tensor(b("g3")[0], b("pb1", 32, 56)[0], b("X3")[0], OP.mult), ["pb1", "X3a", "X3b", "X3c"], ["g3"])
-        tt(b("t3"), b("f3"), b("dvf"), OP.add)
-        tt(b("t1"), b("pb3", 0, 128), b("Mb"), OP.mult)
-        tt(b("oA"), b("g3", 8, 16), b("dmp"), OP.add)
-        cp(b("uvu"), b("oA"))
-        tt(b("q1", 0, 8), b("g3", 0, 8), b("g3", 16, 24), OP.add)
-        ts(b("Bv", 8, 16, key="Bv1"), b("oA"), float(FAR), OP.add)
-        tt(b("t2"), b("pb3", 128, 256), b("xb"), OP.mult)
-        equal("bod", ("pb3", "pb3"), "eqb")
-        ts(b("Dv", 0, 8, key="Dv0"), b("q1", 0, 8), -1.0, OP.mult)
-        tt(b("Bv", 0, 8, key="Bv0"), vf, b("q1", 0, 8), OP.add)
-        tt(b("rsp"), b("w3"), b("t3"), OP.min)
-        cp((b("C")[0].indirect(b("uvu")[0]), ["C", "uvu"]), b("ral"))
+        tt(b("wal"), b("cvf"), b("pb2", 0, 128), OP.max)
+        act(b("f3"), b("w3"), AF.Relu, 8 * 4095.0, -8.0)
+        tt(b("ral"), b("wal"), b("pb2", 128, 256), OP.add)
+        act(b("c0"), b("pb2", 0, 128), AF.Relu, 4095.0, -1.0)
+        act(b("eqb", 0, 512, key="eqb0"), b("pb3"), AF.Relu, -10.0)
+        if s == 2:
+            for k in range(8, 16):
+                act(b("xrep", k, 2048, 16, key="xr"), b("xb"), AF.Copy)
+        tt(b("g3"), b("pb1", 32, 56), b("X3", key=["X3a", "X3b", "X3c"]), OP.mult)
+        tt(b("t1"), b("pb5", 0, 128), b("Mb"), OP.mult)
+        tt(b(tv, 8, 16, key=tv + "u"), b("g3", 8, 16), b("dmp"), OP.add)
+        tt(b("t2"), b("pb5", 128, 256), b("xb"), OP.mult)
+        cp(b("uvu"), b(tv, 8, 16, key=tv + "u"))
+        tt(b("Dv", 0, 8, key="Dv0"), b("g3", 0, 8), b("g3", 16, 24), OP.add)
+        scatter(b("C"), b("uvu"), b("ral"))
+        if t == 1:
+            send_list(s - 1)
         tt(b("An"), b("t1"), b("t2"), OP.add)
-        tt(b("hd"), b("xb"), b("abm"), OP.subtract)
-        tt(b("bd"), b("bf"), b("dmp"), OP.subtract)
-        ts(b("hc1"), b("hd"), 4.5, OP.min, -3.5, OP.max)
-        if s == 0:
-            ms(b("Dv", 8, 16, key="Dv1"), 1.0)
-        tt(b("hv"), b("hc1"), b("abm"), OP.add)
+        tt(b("cb"), b("c0"), b("cvf"), OP.max)
+        tt(b("t3"), b("f3"), b("dvf"), OP.add)
+        ts(b("eqb", 512, 1024, key="eqb1"), b("pb4"), -10.0, OP.add, 0.0, OP.max)
+        tt(b("rsp"), b("w3"), b("t3"), OP.min)
 
         scan(b("fsm"), b("RM2"), b("pb0", 0, 128), OP.max, OP.min)
         tt(b("Sf"), b("fsm", 15, 128, 16), b("Tt"), OP.is_lt)
         act(b("exU"), ind(b("Sf"), bl(8)), AF.Copy)
-        expand("exS", b("Sf"), 1)
         if t == 1:
             tt(b("ov"), b("Sf"), b("anr0"), OP.is_lt)
-            tt(b("hF"), b("Sf"), b("gm3", 0, 8, key="ah"), OP.is_lt)
             ts(b("nov"), b("ov"), 0.0, OP.is_equal, b("p128"), OP.mult)
-        else:
-            tt(b("hF"), b("Sf"), b("gm3", 0, 8, key="ah"), OP.is_lt)
-        to_lists_s = [("sb2", 2), ("sb3", 3)]
-        for j, (key, c) in enumerate(to_lists_s):
-            mm(b("pb1", 56 + 8 * j, 64 + 8 * j), b("exS"), b("sb", 8 * c, 8 * c + 8, key=key))
-        op("v", lambda e: e.tensor_tensor(b("q1")[0], b("pb1", 56, 72)[0], b("Dv")[0], OP.mult), ["pb1", "Dv0", "Dv1"], ["q1"])
+            mm(b("pb3", 8, 16), b("tri"), b("ov"))
+        expand("exS", b("Sf"), 1)
         if t == 1:
-            send_rank()
-        count("eqb", "hF", ("pb3", 0))
-        op("v", lambda e: e.tensor_tensor(b("vf")[0], b("q1")[0], b("Bv")[0], OP.add), ["q1", "Bv0", "Bv1"], ["vf"])
-        cp(b("vu2"), b("vf"))
+            tt(b("pos"), b("pb3", 8, 16), b("nov"), OP.max)
+            expand("exP", b("pos"), 1)
+        tt(b("hF"), b("Sf"), ah, OP.is_lt)
+        mm(b("pb1", 56, 64), one, b("onesb", 0, 8, 1, 0, 1), True, False)
+        mm(b("pb1", 56, 64), b("exS"), b("sb", 0, 8, key="sb0"), False, True)
+        mm(b("pb1", 64, 72), b("exS"), b("sb", 24, 32, key="sb3"))
         if t == 1:
+            to_lists("exP", 1, ("pb1", 80), (2,))
             send_list(s)
-        cp((b("C")[0].indirect(b("vu2", 8, 16)[0]), ["C", "vu2"]), b("rsp"))
-        one = b("onesb", 0, 128, 1, 0, 1)
+        count("eqb", "hF", ("pb3", 0))
+        tt(b("q1"), b("pb1", 56, 72), b("Dv", key=["Dv0", "Dv1"]), OP.mult)
+        tt(b("vf", 0, 16, key="vf"), b("q1"), b(tv, 0, 16, key=[tv, tv + "u"]), OP.add)
+        cp(b("vu2"), b("vf", 0, 16, key="vf"))
+        scatter(b("CW", key="C"), b("vu2", 8, 16), b("rsp"))
         mm(b("pb2", 128, 256), b("exU"), b("GE", 128, 256, key="GE1"), True, False)
         mm(b("pb2", 128, 256), b("exU"), b("m1c"), False, True)
         mm(b("pb2", 0, 128), one, one, True, False)
@@ -549,28 +575,25 @@ def rank_program(g, core, T, topo):
         expand("exH", b("h1"), 1)
         tt(b("C", n0, n0 + L), b("pb2", 128, 256), b("cb"), OP.max)
         to_lists("exH", 1, ("pb1", 72), (2,))
-        tt(b("A", n0, n0 + L), b("pb2", 0, 128), b("An"), OP.mult)
         if s == 3:
             dma("y", "ld5", T.yc[:], b("C", 0, W)[0], ["C"], ["yc"])
+        tt(b("A", n0, n0 + L), b("pb2", 0, 128), b("An"), OP.mult)
         tt(b("oA"), b("pb1", 72, 80), b("bd"), OP.mult)
+        if s < 3:
+            front_v(s + 1, b("tu") if s == 1 else b("vu2", 0, 8))
         tt(b("oA"), b("oA"), b("dmp"), OP.add)
+        if t == 1:
+            tt(b("nF"), b("Sf"), b("an"), OP.is_lt)
         cp(b("oAu"), b("oA"))
-        cp((b("A")[0].indirect(b("oAu")[0]), ["A", "oAu"]), b("hv"))
+        scatter(b("A"), b("oAu"), b("hv"))
         if s == 3:
             dma("y", "ld6", T.ya[:], b("A", 0, W)[0], ["A"], ["ya"])
-        tt(b("nF"), b("Sf"), b("an"), OP.is_lt)
-        if t == 0:
-            tt(b("ov"), b("Sf"), b("anr0"), OP.is_lt)
-            ts(b("nov"), b("ov"), 0.0, OP.is_equal, b("p128"), OP.mult)
-            ts(b("nonr"), b("nF"), 0.0, OP.is_equal)
-            cp(b("rest"), b("nF"))
-        else:
+        if t == 1:
             tt(b("rest2"), b("rest"), b("nF"), OP.add)
             ts(b("nonr2"), b("rest2"), 0.0, OP.is_equal)
 
     def send_rank():
-        mm(b("pb3", 8, 16), b("tri"), b("ov"))
-        tt(b("pos"), b("pb3", 8, 16), b("nov"), OP.max)
+        tt(b("pos"), b("pb1", 96, 104), b("nov"), OP.max)
         expand("exP", b("pos"), 1)
         to_lists("exP", 1, ("pb1", 80), (2,))
 
@@ -578,7 +601,7 @@ def rank_program(g, core, T, topo):
         h = hops(T, topo, rank, s)
         m = "msg%d" % s
         cp(b("posu"), b("pb1", 80, 88))
-        cp((b(m)[0].indirect(b("posu")[0]), [m, "posu"]), b("xp"))
+        scatter(b(m), b("posu"), b("xp"))
         need("g", [m], [])
         n = engines_of(topo, core, h[1])
         rid, pid = topo.addr(h[1], core)
@@ -588,18 +611,14 @@ def rank_program(g, core, T, topo):
             to, sem = T["come%d" % (s // ST)][:, CAP * (s % ST):CAP * (s % ST) + CAP], T.sem["in%d" % s]
         g.remote_dma(to, T[m][:, 0:CAP], sem, T.sem["ls%d" % s], pid, rid, emask(topo, core, h[1], n))
 
-    def arrives(s):
-        src = (rank - 1 - s % (NR - 1)) % NR
-        h = hops(T, topo, src, s)
-        wr["come%d_%d" % (s // ST, s % ST)] = ("remote", "in%d" % s, engines_of(topo, h[-2], h[-1]), {"in%d" % s: engines_of(topo, h[-2], h[-1])})
-        cnt["in%d" % s] = engines_of(topo, h[-2], h[-1])
-
-    for s in range(4):
-        arrives(s)
+    for s in range(ST * RO):
+        h = hops(T, topo, (rank - 1 - s % (NR - 1)) % NR, s)
+        n = engines_of(topo, h[-2], h[-1])
+        wr["come%d_%d" % (s // ST, s % ST)] = ("remote", "in%d" % s, n, {"in%d" % s: n})
+        cnt["in%d" % s] = n
 
     def round_end(s):
-        rnd = s // ST
-        cm = "come%d" % rnd
+        cm = "come%d" % (s // ST)
         mm(b("pb3", 16, 24), b("tri"), b("rest2"), True, False)
         mm(b("pb3", 16, 24), b("I128"), b("nonr2"), False, True)
         tt(b("dM"), ind(b("A", 0, WIN), b("vu2", 0, 8)), b("xb"), OP.subtract)
@@ -609,29 +628,23 @@ def rank_program(g, core, T, topo):
         to_lists("exN", 1, ("pb1", 88), (2,))
         if s == 1:
             front(2, b("tu"))
+            act(b("cvf"), ind(b("C", 0, WIN), b("tu")), AF.Copy)
             for c in range(4):
                 act(b("ag", 512 * c, 512 * c + 512, key="ag%d" % c), ind(b("A", 0, WIN), b("cvu", 32 * c, 32 * c + 32)), AF.Copy)
-        op("v", lambda e: e.tensor_scalar(b("msk")[0], b(cm, 0, CAP)[0], 0.5, None, OP.is_gt), [cm + "_0"], ["msk"])
+        ts(b("msk"), b(cm, 0, CAP, key=cm + "_0"), 0.5, OP.is_gt)
         op("v", lambda e: e.tensor_reduce(b("n0")[0], b("msk")[0], AxisListType.X, OP.add), ["msk"], ["n0"])
         ts(b("cd"), b("n0"), -1.0, OP.mult, float(CAP), OP.add)
         ts(b("ge"), b("pb1", 88, 96), b("n0"), OP.is_ge, b("cd"), OP.mult)
         tt(b("idx"), b("pb1", 88, 96), b("ge"), OP.add)
         ts(b("iu"), b("idx"), 64.0, OP.min)
-        op("v", lambda e: e.tensor_tensor(b("hx")[0], b(cm)[0].indirect(b("iu")[0]), b("ad")[0], OP.max),
-           [cm + "_0", cm + "_1", cm + "z", "iu", "ad"], ["hx"])
+        tt(b("hx"), ind(b(cm, key=[cm + "_0", cm + "_1", cm + "z"]), b("iu")), b("ad"), OP.max)
         ts(b("xi"), b("hx"), 255, OP.bitwise_and)
 
     for s in range(4):
-        t = s % ST
-        if t == 0:
-            step(s, b("tu"), b("topf"))
-            send_rank()
-            send_list(s)
-            if s == 2:
-                for k in range(16):
-                    cp(b("xrep", k, 2048, 16, key="xr"), b("xb"))
+        if s % ST == 0:
+            step(s, b("tu"), "topf")
         else:
-            step(s, b("vu2", 0, 8), b("vf", 0, 8))
+            step(s, b("vu2", 0, 8), "vf")
             round_end(s)
     cp(b("xb"), b("xi"))
     dma("y", "ld7", T.yx[:], b("xb")[0], ["xb"], ["yx"])

@@ -29,7 +29,7 @@ _s("F", CW=FAR + 1680, idf=136, zf=272, RM=272, RM2=128, kcf=408, kcg=408, kpat=
    r=128, y=128, cvf=128, dvf=128, m1=272, m2=272, cand=272, k0s=136, abm=128, sm=128, ym=128, xs=128, xp=128, dM=128,
    hm=8, he=8, nn=8, T0=8, Tt=8, act0=8, an=8, ah0=8, k1=8, k2=8, wal=128, ral=128, w3=128, f3=128, t3=128, v16=8, nv=8,
    rsp=128, c0=128, cb=128, t1=128, t2=128, X3=24, g3=24, gm3=32, Dv=16, q1=16, vf=16, fsm=128, Sf=8, anr0=8, nrm=8, h1=8,
-   oA=8, pos=8, nrs=8, hd=128, hc1=128, ge=8, idx=8, msk=32, n0=1, cd=1, ad=128, mE=1, mO=1, bd=8, p128=1)
+   oA=8, pos=8, nrs=8, am4=128, ap4=128, nGL=32, ge=8, idx=8, msk=32, n0=1, cd=1, ad=128, mE=1, mO=1, bd=8, p128=1, m128=1)
 _s("I", KI=1024, tp=8, thi=128, ci=128, rmi=384, pin=8, pr=8, m16=8, cio=13, bt=143, m1e=16, dec=16, eb=8, kk=24, m2e=16,
    dec2=16, kq=8, hx=128, xi=128, iv=8)
 _s("U", bl=128, tu=8, cvu=128, dvu=128, bu=8, qu=8, uvu=8, vu2=16, oAu=8, posu=8, iu=8)
@@ -55,7 +55,7 @@ def emask(topo, src, dst, n):
     return m
 
 
-NE_ON, NE_OFF = 8, 8
+NE_ON, NE_OFF = 16, 8
 
 
 def hops(T, topo, rank, s):
@@ -109,7 +109,7 @@ def rank_program(g, core, T, topo):
         for k in Wk:
             if k in wr and (wr[k][0] != q or dma):
                 deps.append(wr[k])
-            deps += [d for d in rd.get(k, []) if d[0] != q or dma]
+            deps += [d for d in rd.get(k, []) if d[0] != q or dma or k[:2] == "pb"]
         deps = sorted(deps, key=lambda d: -d[2])
         for d in deps:
             if know[q].get(d[1], 0) < d[2]:
@@ -180,7 +180,7 @@ def rank_program(g, core, T, topo):
         op("v", lambda e: e.tensor_tensor_scan(o[0], a[0], c[0], BIG, f0, f1), ks(a, c), ks(o))
 
     def act(o, a, f, bias=0.0, scale=1.0):
-        op("s", lambda e: e.activation(o[0], a[0], f, bias=bias, scale=ap(scale)), ks(a, scale), ks(o))
+        op("s", lambda e: e.activation(o[0], a[0], f, bias=ap(bias), scale=ap(scale)), ks(a, scale, bias), ks(o))
 
     def mm(o, l, r, start=True, stop=True):
         op("t", lambda e: e.matmul(o[0], l[0], r[0], start, stop), ks(l, r), ks(o))
@@ -247,7 +247,8 @@ def rank_program(g, core, T, topo):
     for h in range(4):
         n = 512 if h < 3 else 128
         act(b("bs", 512 * h, 512 * h + n, 1, 0, 11, key="bs%d" % h), b("pb%d" % (4 + h), 0, n, 1, 0, 11), AF.Copy)
-    for h in range(4):
+
+    def table(h):
         n = 512 if h < 3 else 128
         mm(b("pb%d" % (4 + h), 0, n), b("EE", p1=11), b("bs", 512 * h, 512 * h + n, 1, 0, 11, key="bs%d" % h))
         act(b("Tb", 512 * h, 512 * h + n), b("pb%d" % (4 + h), 0, n), AF.Copy)
@@ -274,8 +275,11 @@ def rank_program(g, core, T, topo):
         ms(b("Dv", 8, 16, key="Dv1"), 1.0)
         tt(b("iGL"), b("pr"), b("m16"), OP.add)
         ts(b("p128"), b("pin", 0, 1), 128.0, OP.add)
+        ts(b("m128"), b("pin", 0, 1), -1.0, OP.mult, -128.0, OP.add)
         ts(b("dmp"), b("iGL"), float(DUMP), OP.add)
         ts(b("dmp16"), b("iGL"), float(DUMP - 1600), OP.add)
+        for k in range(4):
+            ts(b("nGL", 8 * k, 8 * k + 8, key="nGL%d" % k), b("iGL"), float(V0 + L * k), OP.add)
 
     def consts_c():
         cp(b("thf", 0, 128, 1, 0, 8), b("thi", 0, 128, 1, 0, 8))
@@ -286,19 +290,18 @@ def rank_program(g, core, T, topo):
     def consts_d():
         tt(b("Di"), b("idb"), b("ci"), OP.mult)
         ts(b("I128"), b("idb"), 128.0, OP.mult)
-        ts(b("GN", 0, 128, key="GNa"), b("idb"), 8192.0, OP.mult)
         for s in range(4):
-            ts(b("GN", 128 + 128 * s, 256 + 128 * s, key="GN%d" % s), b("idb"), float(128 * (s - 56)), OP.mult)
-        ts(b("GE", 0, 128, key="GE0"), b("idb"), -4096.0, OP.mult)
+            ts(b("GN", 128 + 128 * s, 256 + 128 * s, key="GN%d" % s), b("idb"), float(128 * (s - 24)), OP.mult)
         ts(b("GE", 128, 256, key="GE1"), b("idb"), 4096.0, OP.mult)
         ts(b("m1c"), b("idb"), -1.0, OP.mult)
 
     def x_forms(src):
-        ts(b("xs"), src, MAGIC, OP.add)
-        ts(b("xp"), src, 256.0, OP.add)
+        act(b("xs"), src, AF.Identity, MAGIC)
+        act(b("xp"), src, AF.Identity, 256.0)
 
     def turn_x():
         mm(b("pb3", 0, 128), b("xb"), b("idb"))
+        mm(b("pb1", 384, 512), b("idb"), b("xb"))
         act(b("xT"), b("pb3", 0, 128), AF.Copy)
 
     def preload_x(cs):
@@ -306,8 +309,11 @@ def rank_program(g, core, T, topo):
             mm(b("pb%d" % (4 + c)), b("xT"), b("R", 512 * c, 512 * c + 512), True, False)
 
     def codes_masked(d):
-        ts(b(d + "E"), b(d), b("mE"), OP.mult)
-        ts(b(d + "O"), b(d), b("mO"), OP.mult)
+        for m in "EO":
+            if d == "cod":
+                ts(b(d + m), b(d), b("m" + m), OP.mult)
+            else:
+                act(b(d + m), b(d), AF.Copy, 0.0, b("m" + m))
 
     def equal(d, bank, h):
         mm(b(bank), b("idb"), b("trib"), True, False)
@@ -344,12 +350,27 @@ def rank_program(g, core, T, topo):
         mm(b("pb0", 0, 136), b("r"), b("idf"), False, False)
         mm(b("pb0", 0, 272), b("h8"), b("hc", key=["hc0", "hc1"]), False, False)
 
+    def gather(c):
+        act(b("ag", 512 * c, 512 * c + 512, key="ag%d" % c), ind(b("A", 0, WIN), b("dvu", 32 * c, 32 * c + 32)), AF.Copy)
+
+    def less_x(c):
+        mm(b("pb%d" % (4 + c)), b("idb"), b("ag", 512 * c, 512 * c + 512, key="ag%d" % c), False, True)
+
+    def away(c):
+        act(b("ab2", 512 * c, 512 * c + 512, key="ab2%d" % c), b("pb%d" % (4 + c)), AF.Abs)
+
+    def sums2(l0, l1, cs):
+        for k in range(16):
+            mm(b("pb0", k, 128, 16, l0, l1), b("ab2", 16 * l0 + k, 16 * l1, 16, key=["ab2%d" % c for c in cs]), b("selb"))
+
     def step(s, vu, tv):
         t = s % ST
         n0 = V0 + L * s
         vf = b(tv, 0, 8)
         if s == 0:
             front_v(0, vu)
+            for h in range(4):
+                table(h)
             cp(b("C", 0, V0), b("KI"))
             consts_a()
         if s != 2:
@@ -370,109 +391,97 @@ def rank_program(g, core, T, topo):
             act(dj, dj, AF.Abs)
             if s == 2 and j == 0:
                 turn_x()
-            if j == 0 and s != 2:
-                act(b("cvf"), ind(b("C", 0, WIN), vu), AF.Copy)
-        for l0, l1, js in ((0, 96, (0, 1, 2)), (96, 128, (3, 4))):
+        if s != 2:
+            act(b("cod"), ind(b("Tb", 0, WIN), vu), AF.Copy)
+            act(b("cvf"), ind(b("C", 0, WIN), vu), AF.Copy)
+        for l0, l1, js in ((0, 64, (0, 1)), (64, 96, (2,)), (96, 128, (3, 4))):
             for k in range(16):
                 mm(b("pb0", 1 + k, 272, 17, l0, l1), b("df", 16 * l0 + k, 16 * l1, 16, key=["df%d" % j for j in js]),
                    b("bk", key=["bk0", "bk1"]), False, k == 15)
-        if s != 2:
-            act(b("cod"), ind(b("Tb", 0, WIN), vu), AF.Copy)
         if t == 1:
-            tt(b("nF"), b("Sf"), b("an"), OP.is_lt)
+            tt(b("rest"), b("Sf"), b("an"), OP.is_lt)
             tt(b("ov"), b("Sf"), b("anr0"), OP.is_lt)
-            ts(b("nonr"), b("nF"), 0.0, OP.is_equal)
-            ts(b("nov"), b("ov"), 0.0, OP.is_equal, b("p128"), OP.mult)
-            cp(b("rest"), b("nF"))
+            act(b("nonr"), b("rest"), AF.Identity, 1.0, -1.0)
+            act(b("nov"), b("ov"), AF.Identity, b("p128"), b("m128"))
             mm(b("pb1", 96, 104), b("tri"), b("ov"))
         if s == 0:
             consts_b()
-        if s != 2:
-            codes_masked("cod")
-        ts(b("nv"), b("iGL"), float(n0), OP.add)
         if s in (0, 2):
             x_forms(b("xb"))
+        if s == 2:
+            for k in range(16):
+                cp(b("xrep", k, 2048, 16, key="xr"), b("xb"))
         tt(b("X3", 8, 16, key="X3c"), vf, b("dmp"), OP.subtract)
-        tt(b("X3", 16, 24, key="X3b"), b("nv"), vf, OP.subtract)
-        ts(b("v16"), vf, -1600.0, OP.add)
+        tt(b("X3", 16, 24, key="X3b"), b("nGL", 8 * s, 8 * s + 8, key="nGL%d" % s), vf, OP.subtract)
+        act(b("v16"), vf, AF.Identity, -1600.0)
         scan(b("m1"), b("RM"), b("pb0", 0, 272), OP.max, OP.min)
         cp(b("m1e"), b("m1", 16, 272, 17))
         ts(b("dec"), b("m1e"), 127, OP.bitwise_and)
         expand("ex", b("dec"), 2)
         if s == 2:
             preload_x((0, 1))
-            for k in range(8):
-                act(b("xrep", k, 2048, 16, key="xr"), b("xb"), AF.Copy)
-        else:
-            equal("cod", "pb2", 0)
-            act(b("eqa", 0, 512, key="eqa0"), b("pb2"), AF.Relu, -10.0)
         to_b = b("pb1", 0, 8)
         mm(to_b, b("ex", 0, 128), b("sb", 0, 8, key="sb0"), True, False)
         mm(to_b, b("ex", 128, 256), b("sb", 8, 16, key="sb1"), False, True)
         if s == 2:
             preload_x((2, 3))
         else:
+            codes_masked("cod")
+            equal("cod", "pb2", 0)
             equal("cod", "pb3", 1)
-            act(b("eqa", 512, 1024, key="eqa1"), b("pb3"), AF.Relu, -10.0)
-        if t == 1:
-            send_rank()
-        scan(b("k0s"), b("RM", 0, 136), b("pb0", 272, 408), OP.max, OP.min)
+        tt(b("cand", 1, 272), b("m1", 0, 271), b("pb0", 1, 272), OP.max)
         ts(b("bu"), to_b, 1600.0, OP.add)
         ts(b("dvu"), ind(b("C", 0, WIN), b("bu")), float(E1), OP.min)
-        if s != 2:
-            count("eqa", "nonr" if t == 1 else "one8", ("pb1", 16))
-        act(b("abm"), ind(b("A", 0, WIN), b("bu")), AF.Identity, -0.5)
-        tt(b("cand", 1, 272), b("m1", 0, 271), b("pb0", 1, 272), OP.max)
         tt(b("X3", 0, 8, key="X3a"), to_b, b("v16"), OP.subtract)
-        scan(b("m2", 1, 272), b("RM", 1, 272), b("cand", 1, 272), OP.max, OP.min)
         tt(b("bd"), to_b, b("dmp16"), OP.subtract)
+        act(b("abm"), ind(b("A", 0, WIN), b("bu")), AF.Identity, -0.5)
+        act(b("am4"), b("abm"), AF.Identity, -3.5)
+        act(b("ap4"), b("abm"), AF.Identity, 4.5)
+        gather(0)
+        if s != 2:
+            act(b("eqa", 0, 512, key="eqa0"), b("pb2"), AF.Relu, -10.0)
+            act(b("eqa", 512, 1024, key="eqa1"), b("pb3"), AF.Relu, -10.0)
+        scan(b("m2", 1, 272), b("RM", 1, 272), b("cand", 1, 272), OP.max, OP.min)
         cp(b("m2e"), b("m2", 16, 272, 17))
-        ts(b("eb"), b("m1e", 0, 8), 12, OP.logical_shift_right)
         ts(b("dec2"), b("m2e"), 127, OP.bitwise_and)
-        ts(b("kk", 0, 8, key="kk0"), b("m1e", 0, 8), 7, OP.logical_shift_right, 31, OP.bitwise_and)
         expand("ex2", b("dec2"), 2)
+        ts(b("eb"), b("m1e", 0, 8), 12, OP.logical_shift_right)
+        ts(b("kk", 0, 8, key="kk0"), b("m1e", 0, 8), 7, OP.logical_shift_right, 31, OP.bitwise_and)
+        ts(b("kq"), b("m2e", 0, 8), 7, OP.logical_shift_right, 31, OP.bitwise_and)
         to_q = b("pb1", 8, 16)
         mm(to_q, b("ex2", 0, 128), b("sb", 0, 8, key="sb0"), True, False)
         mm(to_q, b("ex2", 128, 256), b("sb", 8, 16, key="sb1"), False, True)
-        ts(b("kq"), b("m2e", 0, 8), 7, OP.logical_shift_right, 31, OP.bitwise_and)
-        ts(b("nrm"), b("k0s", 16, 136, 17), 16.0, OP.is_gt)
+        scan(b("k0s"), b("RM", 0, 136), b("pb0", 272, 408), OP.max, OP.min)
         ts(b("qu"), to_q, 1600.0, OP.add)
+        if s != 2:
+            count("eqa", "nonr" if t == 1 else "one8", ("pb1", 16))
         tt(b("sm"), ind(b("A", 0, WIN), b("qu")), b("abm"), OP.add)
         if s == 0:
             consts_c()
-        ts(b("ym"), b("sm"), 0.5, OP.mult, MAGIC, OP.add)
-        tt(b("dM"), b("xs"), b("ym"), OP.subtract)
+        ym = b("pb2", 384, 512)
+        ts(ym, b("sm"), 0.5, OP.mult, MAGIC, OP.add)
+        tt(b("dM"), b("xs"), ym, OP.subtract)
+        tt(b("pb1", 256, 384), b("pb1", 384, 512), b("am4"), OP.max)
+        tt(b("hv"), b("pb1", 256, 384), b("ap4"), OP.min)
 
-        def gather(c):
-            act(b("ag", 512 * c, 512 * c + 512, key="ag%d" % c), ind(b("A", 0, WIN), b("dvu", 32 * c, 32 * c + 32)), AF.Copy)
-
-        def less_x(c):
-            mm(b("pb%d" % (4 + c)), b("idb"), b("ag", 512 * c, 512 * c + 512, key="ag%d" % c), False, True)
-
-        def away(c):
-            act(b("ab2", 512 * c, 512 * c + 512, key="ab2%d" % c), b("pb%d" % (4 + c)), AF.Abs)
-
-        gather(0)
         less_x(0)
         act(b("bod"), ind(b("Tb", 0, WIN), b("bu")), AF.Copy)
-        gather(1)
-        less_x(1)
+        act(b("nrm"), b("k0s", 16, 136, 17), AF.Relu, -16.0)
+        codes_masked("bod")
         act(b("absM"), b("dM"), AF.Abs)
         mm(b("pb1", 24, 32), b("absM"), b("selb"))
-        codes_masked("bod")
+        gather(1)
+        less_x(1)
         equal("bod", "pb3", 0)
         away(0)
+        if s != 2:
+            equal("bod", "pb4", 1)
         gather(2)
-        less_x(2)
-        act(b("Mb"), b("ym"), AF.Identity, -MAGIC)
+        act(b("Mb"), ym, AF.Identity, -MAGIC)
         away(1)
         gather(3)
         act(b("dvf"), ind(b("C", 0, WIN), b("bu")), AF.Copy)
-        away(2)
 
-        tt(b("hd"), b("xb"), b("abm"), OP.subtract)
-        ts(b("hc1"), b("hd"), 4.5, OP.min, -3.5, OP.max)
-        tt(b("hv"), b("hc1"), b("abm"), OP.add)
         ac = b("gm3", 8, 16, key="ac")
         if s == 2:
             cp(ac, b("act0"))
@@ -501,36 +510,39 @@ def rank_program(g, core, T, topo):
         if s == 0:
             consts_d()
         ohb, ohn, ohe = b("oh", 0, 128), b("oh", 128, 256), b("oh", 256, 384)
-        i8 = b("GN", 0, 128, key="GNa")
+        i8 = b("GE", 128, 256, key="GE1")
         mm(b("pb2", 256, 384), ohb, i8)
         mm(b("pb2", 0, 128), ohn, i8, True, False)
         mm(b("pb2", 0, 128), ohe, i8, False, True)
         mm(b("pb2", 128, 256), ohn, b("GN", 128 + 128 * s, 256 + 128 * s, key="GN%d" % s), True, False)
         mm(b("pb2", 128, 256), ohn, b("Di"), False, False)
-        mm(b("pb2", 128, 256), ohe, b("GE", 0, 128, key="GE0"), False, False)
         mm(b("pb2", 128, 256), ohe, b("m1c"), False, True)
+        less_x(2)
+        act(b("gx"), ind(b("gm3", 16, 32, key=["am", "ax"]), bl(16)), AF.Copy)
+        away(2)
+        if t == 1:
+            send_rank()
         tt(b("gm"), ind(b("gm3", 0, 24, key=["ah", "ac", "am"]), bl(24)), b("rmask"), OP.mult)
         to_lists("gm", 3, ("pb1", 32), (2, 2, 2))
-        less_x(3)
-        act(b("gx"), ind(b("gm3", 16, 32, key=["am", "ax"]), bl(16)), AF.Copy)
-        away(3)
+        if t == 1:
+            to_lists("exP", 1, ("pb1", 80), (2,))
         mm(b("pb5", 0, 128), b("gx", 0, 128), b("idb"))
         mm(b("pb5", 128, 256), b("gx", 128, 256), b("idb"))
-        equal("bod", "pb4", 1)
-        for l0, l1, cs in ((0, 96, (0, 1, 2)), (96, 128, (3,))):
-            for k in range(16):
-                mm(b("pb0", k, 128, 16, l0, l1), b("ab2", 16 * l0 + k, 16 * l1, 16, key=["ab2%d" % c for c in cs]), b("selb"))
+        less_x(3)
+        sums2(0, 96, (0, 1, 2))
+        away(3)
+        sums2(96, 128, (3,))
+        if s == 2:
+            equal("bod", "pb4", 1)
         tt(b("w3"), b("cvf"), b("pb2", 256, 384), OP.max)
         tt(b("wal"), b("cvf"), b("pb2", 0, 128), OP.max)
-        act(b("f3"), b("w3"), AF.Relu, 8 * 4095.0, -8.0)
+        act(b("pb6", 0, 128), b("w3"), AF.Relu, 8 * 4095.0, -8.0)
         tt(b("ral"), b("wal"), b("pb2", 128, 256), OP.add)
-        act(b("c0"), b("pb2", 0, 128), AF.Relu, 4095.0, -1.0)
+        act(b("pb7", 0, 128), b("pb2", 0, 128), AF.Relu, 4095.0, -1.0)
         act(b("eqb", 0, 512, key="eqb0"), b("pb3"), AF.Relu, -10.0)
-        if s == 2:
-            for k in range(8, 16):
-                act(b("xrep", k, 2048, 16, key="xr"), b("xb"), AF.Copy)
+        act(b("eqb", 512, 1024, key="eqb1"), b("pb4"), AF.Relu, -10.0)
         tt(b("g3"), b("pb1", 32, 56), b("X3", key=["X3a", "X3b", "X3c"]), OP.mult)
-        tt(b("t1"), b("pb5", 0, 128), b("Mb"), OP.mult)
+        tt(b("pb5", 256, 384), b("pb5", 0, 128), b("Mb"), OP.mult)
         tt(b(tv, 8, 16, key=tv + "u"), b("g3", 8, 16), b("dmp"), OP.add)
         tt(b("t2"), b("pb5", 128, 256), b("xb"), OP.mult)
         cp(b("uvu"), b(tv, 8, 16, key=tv + "u"))
@@ -538,11 +550,8 @@ def rank_program(g, core, T, topo):
         scatter(b("C"), b("uvu"), b("ral"))
         if t == 1:
             send_list(s - 1)
-        tt(b("An"), b("t1"), b("t2"), OP.add)
-        tt(b("cb"), b("c0"), b("cvf"), OP.max)
-        tt(b("t3"), b("f3"), b("dvf"), OP.add)
-        ts(b("eqb", 512, 1024, key="eqb1"), b("pb4"), -10.0, OP.add, 0.0, OP.max)
-        tt(b("rsp"), b("w3"), b("t3"), OP.min)
+        tt(b("pb5", 384, 512), b("pb6", 0, 128), b("dvf"), OP.add)
+        tt(b("rsp"), b("w3"), b("pb5", 384, 512), OP.min)
 
         scan(b("fsm"), b("RM2"), b("pb0", 0, 128), OP.max, OP.min)
         tt(b("Sf"), b("fsm", 15, 128, 16), b("Tt"), OP.is_lt)
@@ -561,8 +570,13 @@ def rank_program(g, core, T, topo):
         mm(b("pb1", 64, 72), b("exS"), b("sb", 24, 32, key="sb3"))
         if t == 1:
             to_lists("exP", 1, ("pb1", 80), (2,))
+            tt(b("An"), b("pb5", 256, 384), b("t2"), OP.add)
+            tt(b("cb"), b("pb7", 0, 128), b("cvf"), OP.max)
             send_list(s)
         count("eqb", "hF", ("pb3", 0))
+        if t == 0:
+            tt(b("An"), b("pb5", 256, 384), b("t2"), OP.add)
+            tt(b("cb"), b("pb7", 0, 128), b("cvf"), OP.max)
         tt(b("q1"), b("pb1", 56, 72), b("Dv", key=["Dv0", "Dv1"]), OP.mult)
         tt(b("vf", 0, 16, key="vf"), b("q1"), b(tv, 0, 16, key=[tv, tv + "u"]), OP.add)
         cp(b("vu2"), b("vf", 0, 16, key="vf"))
@@ -590,12 +604,11 @@ def rank_program(g, core, T, topo):
             dma("y", "ld6", T.ya[:], b("A", 0, W)[0], ["A"], ["ya"])
         if t == 1:
             tt(b("rest2"), b("rest"), b("nF"), OP.add)
-            ts(b("nonr2"), b("rest2"), 0.0, OP.is_equal)
+            act(b("nonr2"), b("rest2"), AF.Identity, 1.0, -1.0)
 
     def send_rank():
         tt(b("pos"), b("pb1", 96, 104), b("nov"), OP.max)
         expand("exP", b("pos"), 1)
-        to_lists("exP", 1, ("pb1", 80), (2,))
 
     def send_list(s):
         h = hops(T, topo, rank, s)
@@ -630,7 +643,11 @@ def rank_program(g, core, T, topo):
             front(2, b("tu"))
             act(b("cvf"), ind(b("C", 0, WIN), b("tu")), AF.Copy)
             for c in range(4):
-                act(b("ag", 512 * c, 512 * c + 512, key="ag%d" % c), ind(b("A", 0, WIN), b("cvu", 32 * c, 32 * c + 32)), AF.Copy)
+                o, a = b("ag", 512 * c, 512 * c + 512, key="ag%d" % c), ind(b("A", 0, WIN), b("cvu", 32 * c, 32 * c + 32))
+                if c < 3:
+                    act(o, a, AF.Copy)
+                else:
+                    cp(o, a)
         ts(b("msk"), b(cm, 0, CAP, key=cm + "_0"), 0.5, OP.is_gt)
         op("v", lambda e: e.tensor_reduce(b("n0")[0], b("msk")[0], AxisListType.X, OP.add), ["msk"], ["n0"])
         ts(b("cd"), b("n0"), -1.0, OP.mult, float(CAP), OP.add)

from concourse.mybir import AluOpType as OP, ActivationFunctionType as AF, AxisListType

V0, L, ST, RO, CAP, NR = 1024, 128, 2, 2, 32, 8
W = V0 + RO * ST * L
E1 = W
WIN = W + 8
DUMP = WIN
FAR = 2048
BIG = float(2 ** 30)
MAGIC = float(2 ** 23)
PIECES = [(0, 32), (32, 32), (64, 32), (96, 16), (112, 16)]

SLOT = {}
SIZE = {"F": 0, "B": 0, "I": 0, "U": 0}


def _s(kind, **kw):
    for n, w in kw.items():
        SLOT[n] = ("ar" + kind, SIZE[kind], w)
        SIZE[kind] += (w + 15) // 16 * 16


_s("B", A=1680, xrep=2048, df=2048, ag=2048, ab2=2048, xb=128, xT=128, R=2048, onesb=512, zb=512, idb=128, ipb=136,
   hc=272, f16p=136, selb=8, sel2=8, bk=16, sb=32, tri=128, trib=512, kcb=408, rmask=384, Di=128, I128=128, GN=640, GE=256,
   m1c=128, bb=143, bs=1664, EE=128, Tb=1664, h8=128, Fm=128, cod=128, codE=128, codO=128, bod=128, bodE=128, bodO=128,
   eqa=1024, eqb=1024, ex=256, ex2=256, oh=384, gx=256, gm=384, exS=128, exU=128, exH=128, exP=128, exN=128, absM=128, Mb=128,
   An=128, hv=128, hF=8, ov=8, nov=8, rest=8, rest2=8, nonr=8, nonr2=8, one8=8, nF=8)
_s("F", CW=FAR + 1680, idf=136, zf=272, RM=272, RM2=128, kcf=408, kcg=408, kpat=384, iGL=8, dmp=8, dmp16=8, lim=8, lim1=8, thf=128, topf=16,
   r=128, y=128, cvf=128, dvf=128, m1=272, m2=272, cand=272, k0s=136, abm=128, sm=128, ym=128, xs=128, xp=128, dM=128,
   hm=8, he=8, nn=8, T0=8, Tt=8, act0=8, an=8, ah0=8, k1=8, k2=8, wal=128, ral=128, w3=128, f3=128, t3=128, v16=8, nv=8,
   rsp=128, c0=128, cb=128, t1=128, t2=128, X3=24, g3=24, gm3=32, Dv=16, q1=16, vf=16, fsm=128, Sf=8, anr0=8, nrm=8, h1=8,
   oA=8, pos=8, nrs=8, am4=128, ap4=128, nGL=32, ge=8, idx=8, msk=32, n0=1, cd=1, ad=128, mE=1, mO=1, bd=8, p128=1, m128=1)
_s("I", KI=1024, tp=8, thi=128, ci=128, rmi=384, pin=8, pr=8, m16=8, cio=13, bt=143, m1e=16, dec=16, eb=8, kk=24, m2e=16,
   dec2=16, kq=8, hx=128, xi=128, iv=8)
_s("U", bl=128, tu=8, cvu=128, dvu=128, bu=8, qu=8, uvu=8, vu2=16, oAu=8, posu=8, iu=8)
SLOT["C"] = ("arF", SLOT["CW"][1] + FAR, 1680)

SCRATCH = {"arF": ("sbuf", [128, SIZE["F"]], "float32"), "arB": ("sbuf", [128, SIZE["B"]], "bfloat16"),
           "arI": ("sbuf", [128, SIZE["I"]], "int32"), "arU": ("sbuf", [128, SIZE["U"]], "uint16")}
for _k in range(8):
    SCRATCH["pb%d" % _k] = ("psum", [128, 512], "float32")
for _k in range(4):
    SCRATCH["msg%d" % _k] = ("sbuf", [128, 256], "float32")
    SCRATCH["rl%d" % _k] = ("sbuf", [128, 32], "float32")
for _k in range(2):
    SCRATCH["come%d" % _k] = ("sbuf", [128, 80], "float32")
SEMAPHORES = (["qv", "qs", "qt", "qg"] + ["in%d" % k for k in range(4)] + ["rr%d" % k for k in range(4)] + ["ls%d" % k for k in range(4)]
              + ["ld%d" % k for k in range(8)])


def emask(topo, src, dst, n):
    m = 0
    for e in topo.engines(src, dst)[:n]:
        m |= 1 << e
    return m


NE_ON, NE_OFF = 16, 8


def hops(T, topo, rank, s):
    src, dst = T.cores[rank], T.cores[(rank + 1 + s % (NR - 1)) % NR]
    if s > 0 and topo.may_write(src, dst):
        return [src, dst]
    ways = [c for c in topo.cores_of(src) if c != src and all(topo.may_write(c, d) for d in T.cores if d not in topo.cores_of(src))]
    ways.sort(key=lambda c: topo.die(c) != topo.die(src))
    return [src, ways[0], dst]


def engines_of(topo, a, b):
    return NE_ON if b in topo.cores_of(a) else NE_OFF


def relay(g, core, T, topo):
    for s in range(ST * RO):
        for rank in range(NR):
            h = hops(T, topo, rank, s)
            if len(h) == 3 and h[1] == core:
                n = engines_of(topo, h[1], h[2])
                g.wait_ge(T.sem["rr%d" % s], engines_of(topo, h[0], core))
                rid, pid = topo.addr(h[2], core)
                g.remote_dma(T["come%d" % (s // ST)][:, CAP * (s % ST):CAP * (s % ST) + CAP], T["rl%d" % s][:, 0:CAP], T.sem["in%d" % s],
                             T.sem["ls%d" % s], pid, rid, emask(topo, core, h[2], n))
    for s in range(ST * RO):
        for rank in range(NR):
            h = hops(T, topo, rank, s)
            if len(h) == 3 and h[1] == core:
                g.wait_ge(T.sem["ls%d" % s], engines_of(topo, h[1], h[2]))


def rank_program(g, core, T, topo):
    rank = T.rank_of(core)
    if rank is None:
        relay(g, core, T, topo)
        return
    eng = {"v": g.vector, "s": g.scalar, "t": g.tensor, "g": g, "y": g.sync}
    own = {"v": "qv", "s": "qs", "t": "qt", "g": "qg"}
    cnt = {"qv": 0, "qs": 0, "qt": 0, "qg": 0}
    know = {q: {} for q in eng}
    wr, rd = {}, {}

    def need(q, R, Wk, dma=False):
        deps = []
        for k in R:
            if k in wr:
                deps.append(wr[k])
            if k[:2] == "pb":
                deps += [d for d in rd.get(k, []) if d[0] != q]
        for k in Wk:
            if k in wr and (wr[k][0] != q or dma):
                deps.append(wr[k])
            deps += [d for d in rd.get(k, []) if d[0] != q or dma or k[:2] == "pb"]
        deps = sorted(deps, key=lambda d: -d[2])
        for d in deps:
            if know[q].get(d[1], 0) < d[2]:
                eng[q].wait_ge(T.sem[d[1]], d[2])
                for n, v in d[3].items():
                    know[q][n] = max(know[q].get(n, 0), v)

    def note(tag, sem, val, snap, R, Wk):
        snap = dict(snap)
        snap[sem] = val
        d = (tag, sem, val, snap)
        for k in R:
            rd.setdefault(k, []).append(d)
            rd[k] = [e for e in rd[k] if e is d or e[0] != tag or e[1] != sem]
        for k in Wk:
            wr[k] = d
            rd[k] = []

    def op(q, call, R, Wk):
        need(q, R, Wk)
        s = own[q]
        cnt[s] += 1
        call(eng[q]).then_inc(T.sem[s], 1)
        note(q, s, cnt[s], know[q], R, Wk)

    def dma(q, sem, out, in_, R, Wk):
        need(q, R, Wk, True)
        eng[q].dma_start(out, in_).then_inc(T.sem[sem], 16)
        cnt[sem] = 16
        note("dma" + sem, sem, 16, know[q], R, Wk)

    def b(name, c0=0, c1=None, st=1, p0=0, p1=128, key=None):
        if name in SLOT:
            buf, o, w = SLOT[name]
        else:
            buf, o, w = name, 0, SCRATCH[name][1][1]
        c1 = w if c1 is None else c1
        return (T[buf][p0:p1, o + c0:o + c1:st] if st != 1 else T[buf][p0:p1, o + c0:o + c1], key if isinstance(key, list) else [key or name])

    def ind(win, off):
        return (win[0].indirect(off[0]), win[1] + off[1])

    def ks(*refs):
        return [k for r in refs if isinstance(r, tuple) for k in r[1]]

    def ap(x):
        return x[0] if isinstance(x, tuple) else x

    def tt(o, a, c, f):
        op("v", lambda e: e.tensor_tensor(o[0], a[0], c[0], f), ks(a, c), ks(o))

    def ts(o, a, s1, f0, s2=None, f1=None):
        if f1 is None:
            op("v", lambda e: e.tensor_scalar(o[0], a[0], ap(s1), None, f0), ks(a, s1), ks(o))
        else:
            op("v", lambda e: e.tensor_scalar(o[0], a[0], ap(s1), ap(s2), f0, f1), ks(a, s1, s2), ks(o))

    def cp(o, a):
        op("v", lambda e: e.tensor_copy(o[0], a[0]), ks(a), ks(o))

    def scatter(win, off, a):
        op("v", lambda e: e.tensor_copy(win[0].indirect(off[0]), a[0]), ks(a, off), ks(win))

    def ms(o, v):
        op("v", lambda e: e.memset(o[0], v), [], ks(o))

    def scan(o, a, c, f0, f1):
        op("v", lambda e: e.tensor_tensor_scan(o[0], a[0], c[0], BIG, f0, f1), ks(a, c), ks(o))

    def act(o, a, f, bias=0.0, scale=1.0):
        op("s", lambda e: e.activation(o[0], a[0], f, bias=ap(bias), scale=ap(scale)), ks(a, scale, bias), ks(o))

    def mm(o, l, r, start=True, stop=True):
        op("t", lambda e: e.matmul(o[0], l[0], r[0], start, stop), ks(l, r), ks(o))

    def io(o, pat, base, cm, flag=False):
        if flag:
            op("g", lambda e: e.iota(o[0], pat, base, cm, allow_small_or_imprecise_dtypes=True), [], ks(o))
        else:
            op("g", lambda e: e.iota(o[0], pat, base, cm), [], ks(o))

    def asel(o, a, pat, f, fill, base, cm):
        op("g", lambda e: e.affine_select(o[0], a[0], pat, f, fill, base, cm), ks(a), ks(o))

    bl = lambda n, c0=0: b("bl", c0, c0 + n)
    one = b("onesb", 0, 128, 1, 0, 1)

    dma("y", "ld0", b("tp")[0], T.tops[:], [], ["tp"])
    dma("y", "ld1", b("xb")[0], T.x0[:], [], ["xb"])
    dma("y", "ld2", b("KI")[0], T.kids[:], [], ["KI"])
    dma("s", "ld4", b("thi", 0, 128, 1, 0, 8)[0], T.th[:], [], ["thi"])
    ms(b("A", V0, W), 0.0)
    ms(b("A", W, WIN), 4096.0)
    dma("y", "ld3", b("A", 0, V0)[0], T.a0[:], [], ["A"])
    ms(b("onesb"), 1.0)
    ms(b("zf"), 0.0)
    ms(b("zb"), 0.0)
    for k in range(2):
        ms(b("come%d" % k, 64, 80, key="come%dz" % k), 0.0)
    for k in range(4):
        ms(b("msg%d" % k, 0, CAP), 0.0)
    io(b("cio"), [[128, 13]], 0, 1)
    io(b("ci"), [[1, 128]], 0, 0)
    asel(b("idb"), b("onesb", 0, 128), [[-1, 128]], OP.is_equal, 0.0, 0, 1)
    asel(b("EE", p1=16), b("onesb", 0, 128, 1, 0, 16), [[0, 8], [-1, 16]], OP.is_equal, 0.0, 0, 1)
    asel(b("ipb"), b("onesb", 0, 136), [[-16, 8], [-1, 17]], OP.is_equal, 0.0, 1, 1)
    io(b("kcf", 0, 136, key="kcf0"), [[0, 8], [128, 17]], 64, 0, True)
    io(b("kcf", 136, 272, key="kcf1"), [[0, 8], [128, 17]], 0, 0, True)
    io(b("kcf", 272, 408, key="kcf2"), [[0, 8], [1, 17]], 0, 0, True)
    asel(b("kcg"), b("kcf", key=["kcf0", "kcf1", "kcf2"]), [[0, 24], [1, 17]], OP.not_equal, BIG, 0, 0)
    asel(b("sel2"), b("onesb", 0, 8), [[-16, 8]], OP.is_ge, 0.0, 0, 1)
    asel(b("selb"), b("sel2"), [[16, 8]], OP.is_ge, 0.0, 15, -1)
    io(b("pin"), [[0, 8]], 0, 1)
    io(b("m16"), [[16, 8]], 0, 0)
    asel(b("RM"), b("zf"), [[0, 16], [1, 17]], OP.not_equal, BIG, 0, 0)
    io(b("rmi"), [[0, 24], [-1, 16]], 16, 1)
    asel(b("trib"), b("zb"), [[0, 4], [1, 128]], OP.is_gt, -32.0, 0, -1)
    io(b("kpat"), [[0, 24], [1, 16]], 1, 0, True)
    asel(b("tri"), b("onesb", 0, 128), [[1, 128]], OP.is_gt, 0.0, 0, -1)
    asel(b("RM2"), b("zf", 0, 128), [[0, 8], [1, 16]], OP.not_equal, BIG, 0, 0)

    ms(b("C", V0, WIN), 4095.0)
    for k in range(11):
        ts(b("bt", 13 * k, 13 * k + 13, key="bt"), b("cio"), k, OP.logical_shift_right, 1, OP.bitwise_and)
    ts(b("bb"), b("bt"), 2.0, OP.mult, -1.0, OP.add)
    cp(b("bl"), b("ci"))
    cp(b("tu"), b("tp"))
    cp(b("topf", 0, 8, key="topf"), b("tp"))
    for k in range(16):
        cp(b("xrep", k, 2048, 16, key="xr"), b("xb"))
    for k in range(16):
        act(b("R", k, 2048, 16, key="R"), b("idb"), AF.Copy, 0.0, -1.0)
    for q in range(13):
        mm(b("pb%d" % (4 + q // 4), 128 * (q % 4), 128 * (q % 4) + 128, 1, 0, 11), b("bb", q, 143, 13), b("idb"))
    for h in range(4):
        n = 512 if h < 3 else 128
        act(b("bs", 512 * h, 512 * h + n, 1, 0, 11, key="bs%d" % h), b("pb%d" % (4 + h), 0, n, 1, 0, 11), AF.Copy)

    def table(h):
        n = 512 if h < 3 else 128
        mm(b("pb%d" % (4 + h), 0, n), b("EE", p1=11), b("bs", 512 * h, 512 * h + n, 1, 0, 11, key="bs%d" % h))
        act(b("Tb", 512 * h, 512 * h + n), b("pb%d" % (4 + h), 0, n), AF.Copy)

    def consts_a():
        cp(b("idf"), b("ipb"))
        ts(b("hc", 0, 136, key="hc0"), b("ipb"), -16.0, OP.mult)
        cp(b("hc", 136, 272, key="hc1"), b("ipb"))
        ts(b("f16p"), b("ipb"), 16.0, OP.mult)
        cp(b("kcb"), b("kcg"))
        ts(b("bk", 0, 8, key="bk0"), b("selb"), 4096.0, OP.mult)
        ts(b("bk", 8, 16, key="bk1"), b("selb"), 4096.0, OP.mult)

    def consts_b():
        ts(b("iv"), b("pin"), 4, OP.logical_shift_right, 1, OP.bitwise_and)
        for j, m in enumerate((-1.0, -16.0, 1.0, float(FAR))):
            ts(b("sb", 8 * j, 8 * j + 8, key="sb%d" % j), b("selb"), m, OP.mult)
        ts(b("rmi"), b("rmi"), 15, OP.bitwise_and)
        cp(b("mO"), b("iv", 0, 1))
        ts(b("mE"), b("iv", 0, 1), -1.0, OP.mult, 1.0, OP.add)
        ts(b("rmask"), b("rmi"), 0.0, OP.is_equal)
        ts(b("pr"), b("pin"), 15, OP.bitwise_and)
        ms(b("one8"), 1.0)
        ms(b("Dv", 8, 16, key="Dv1"), 1.0)
        tt(b("iGL"), b("pr"), b("m16"), OP.add)
        ts(b("p128"), b("pin", 0, 1), 128.0, OP.add)
        ts(b("m128"), b("pin", 0, 1), -1.0, OP.mult, -128.0, OP.add)
        ts(b("dmp"), b("iGL"), float(DUMP), OP.add)
        ts(b("dmp16"), b("iGL"), float(DUMP - 1600), OP.add)
        for k in range(4):
            ts(b("nGL", 8 * k, 8 * k + 8, key="nGL%d" % k), b("iGL"), float(V0 + L * k), OP.add)

    def consts_c():
        cp(b("thf", 0, 128, 1, 0, 8), b("thi", 0, 128, 1, 0, 8))
        mm(b("pb3", 0, 8), b("thf", 0, 128, 1, 0, 8), b("idf", 1, 9, 1, 0, 8))
        cp(b("lim"), b("pb3", 0, 8))
        ts(b("lim1"), b("lim"), 1.0, OP.add)

    def consts_d():
        tt(b("Di"), b("idb"), b("ci"), OP.mult)
        ts(b("I128"), b("idb"), 128.0, OP.mult)
        for s in range(4):
            ts(b("GN", 128 + 128 * s, 256 + 128 * s, key="GN%d" % s), b("idb"), float(128 * (s - 24)), OP.mult)
        ts(b("GE", 128, 256, key="GE1"), b("idb"), 4096.0, OP.mult)
        ts(b("m1c"), b("idb"), -1.0, OP.mult)

    def x_forms(src):
        act(b("xs"), src, AF.Identity, MAGIC)
        act(b("xp"), src, AF.Identity, 256.0)

    def turn_x():
        mm(b("pb3", 0, 128), b("xb"), b("idb"))
        mm(b("pb1", 384, 512), b("idb"), b("xb"))
        act(b("xT"), b("pb3", 0, 128), AF.Copy)

    def preload_x(cs):
        for c in cs:
            mm(b("pb%d" % (4 + c)), b("xT"), b("R", 512 * c, 512 * c + 512), True, False)

    def codes_masked(d):
        for m in "EO":
            if d == "cod":
                ts(b(d + m), b(d), b("m" + m), OP.mult)
            else:
                act(b(d + m), b(d), AF.Copy, 0.0, b("m" + m))

    def equal(d, bank, h):
        mm(b(bank), b("idb"), b("trib"), True, False)
        for j in range(4):
            w = 4 * h + j
            p = w // 2 * 32
            if j == 2:
                need("t", [bank], [])
            mm(b(bank, 128 * j, 128 * j + 128), b(d, 0, 128, 1, p, p + 32), b(d + ("O" if w % 2 else "E"), 0, 128, 1, p, p + 32),
               False, j == 3)

    def count(eq, mask, o):
        for w in range(8):
            mm(b(o[0], o[1] + w, o[1] + w + 1), b(eq, 128 * w, 128 * w + 128, key=eq + str(w // 4)), b(mask, w, w + 1))

    def to_lists(ex, n, o, scales):
        for j in range(n):
            mm(b(o[0], o[1] + 8 * j, o[1] + 8 * j + 8), b(ex, 128 * j, 128 * j + 128), b("sb", 8 * scales[j], 8 * scales[j] + 8, key="sb%d" % scales[j]))

    def expand(ex, src, n):
        tt(b(ex, 0, 128 * n), ind(src, bl(8 * n)), b("rmask", 0, 128 * n), OP.mult)

    def front_v(s, vu):
        ts(b("cvu"), ind(b("KI") if s == 0 else b("C", 0, WIN), vu), float(E1), OP.min)

    def front(s, vu):
        act(b("r"), ind(b("C", 0, WIN), vu), AF.Relu, float(E1), -1.0)
        act(b("y"), b("r"), AF.Identity, MAGIC, 1.0 / 127.95)
        act(b("h8"), b("y"), AF.Identity, -8 * MAGIC, 8.0)
        act(b("Fm"), b("r"), AF.Sign)
        mm(b("pb0", 272, 408), one, b("kcb", 272, 408, 1, 0, 1), True, False)
        mm(b("pb0", 272, 408), b("Fm"), b("f16p"), False, True)
        mm(b("pb0", 0, 272), one, b("kcb", 0, 272, 1, 0, 1), True, False)
        mm(b("pb0", 0, 136), b("r"), b("idf"), False, False)
        mm(b("pb0", 0, 272), b("h8"), b("hc", key=["hc0", "hc1"]), False, False)

    def gather(c):
        act(b("ag", 512 * c, 512 * c + 512, key="ag%d" % c), ind(b("A", 0, WIN), b("dvu", 32 * c, 32 * c + 32)), AF.Copy)

    def less_x(c):
        mm(b("pb%d" % (4 + c)), b("idb"), b("ag", 512 * c, 512 * c + 512, key="ag%d" % c), False, True)

    def away(c):
        act(b("ab2", 512 * c, 512 * c + 512, key="ab2%d" % c), b("pb%d" % (4 + c)), AF.Abs)

    def sums2(l0, l1, cs):
        for k in range(16):
            mm(b("pb0", k, 128, 16, l0, l1), b("ab2", 16 * l0 + k, 16 * l1, 16, key=["ab2%d" % c for c in cs]), b("selb"))

    def step(s, vu, tv):
        t = s % ST
        n0 = V0 + L * s
        vf = b(tv, 0, 8)
        if s == 0:
            front_v(0, vu)
            for h in range(4):
                table(h)
            cp(b("C", 0, V0), b("KI"))
            consts_a()
        if s != 2:
            front(s, vu)
        if s == 0:
            turn_x()
        if s != 2:
            preload_x((0, 1, 2, 3))
        for j, (l0, n) in enumerate(PIECES):
            c0, c1 = 16 * l0, 16 * (l0 + n)
            dj = b("df", c0, c1, key="df%d" % j)
            if s == 2:
                tt(dj, ind(b("xi"), bl(n, l0)), b("ag", c0, c1, key="ag%d" % (l0 // 32)), OP.subtract)
                if j == 0:
                    cp(b("xb"), b("xi"))
            else:
                tt(dj, ind(b("A", 0, WIN), b("cvu", l0, l0 + n)), b("xrep", c0, c1, key="xr"), OP.subtract)
            act(dj, dj, AF.Abs)
            if s == 2 and j == 0:
                turn_x()
        if s != 2:
            act(b("cod"), ind(b("Tb", 0, WIN), vu), AF.Copy)
            act(b("cvf"), ind(b("C", 0, WIN), vu), AF.Copy)
        for l0, l1, js in ((0, 64, (0, 1)), (64, 96, (2,)), (96, 128, (3, 4))):
            for k in range(16):
                mm(b("pb0", 1 + k, 272, 17, l0, l1), b("df", 16 * l0 + k, 16 * l1, 16, key=["df%d" % j for j in js]),
                   b("bk", key=["bk0", "bk1"]), False, k == 15)
        if t == 1:
            tt(b("rest"), b("Sf"), b("an"), OP.is_lt)
            tt(b("ov"), b("Sf"), b("anr0"), OP.is_lt)
            act(b("nonr"), b("rest"), AF.Identity, 1.0, -1.0)
            act(b("nov"), b("ov"), AF.Identity, b("p128"), b("m128"))
            mm(b("pb1", 96, 104), b("tri"), b("ov"))
        if s == 0:
            consts_b()
        if s in (0, 2):
            x_forms(b("xb"))
        if s == 2:
            for k in range(16):
                cp(b("xrep", k, 2048, 16, key="xr"), b("xb"))
        tt(b("X3", 8, 16, key="X3c"), vf, b("dmp"), OP.subtract)
        tt(b("X3", 16, 24, key="X3b"), b("nGL", 8 * s, 8 * s + 8, key="nGL%d" % s), vf, OP.subtract)
        act(b("v16"), vf, AF.Identity, -1600.0)
        scan(b("m1"), b("RM"), b("pb0", 0, 272), OP.max, OP.min)
        cp(b("m1e"), b("m1", 16, 272, 17))
        ts(b("dec"), b("m1e"), 127, OP.bitwise_and)
        expand("ex", b("dec"), 2)
        if s == 2:
            preload_x((0, 1))
        to_b = b("pb1", 0, 8)
        mm(to_b, b("ex", 0, 128), b("sb", 0, 8, key="sb0"), True, False)
        mm(to_b, b("ex", 128, 256), b("sb", 8, 16, key="sb1"), False, True)
        if s == 2:
            preload_x((2, 3))
        else:
            codes_masked("cod")
            equal("cod", "pb2", 0)
            equal("cod", "pb3", 1)
        tt(b("cand", 1, 272), b("m1", 0, 271), b("pb0", 1, 272), OP.max)
        ts(b("bu"), to_b, 1600.0, OP.add)
        ts(b("dvu"), ind(b("C", 0, WIN), b("bu")), float(E1), OP.min)
        tt(b("X3", 0, 8, key="X3a"), to_b, b("v16"), OP.subtract)
        tt(b("bd"), to_b, b("dmp16"), OP.subtract)
        act(b("abm"), ind(b("A", 0, WIN), b("bu")), AF.Identity, -0.5)
        act(b("am4"), b("abm"), AF.Identity, -3.5)
        act(b("ap4"), b("abm"), AF.Identity, 4.5)
        gather(0)
        if s != 2:
            act(b("eqa", 0, 512, key="eqa0"), b("pb2"), AF.Relu, -10.0)
            act(b("eqa", 512, 1024, key="eqa1"), b("pb3"), AF.Relu, -10.0)
        scan(b("m2", 1, 272), b("RM", 1, 272), b("cand", 1, 272), OP.max, OP.min)
        cp(b("m2e"), b("m2", 16, 272, 17))
        ts(b("dec2"), b("m2e"), 127, OP.bitwise_and)
        expand("ex2", b("dec2"), 2)
        ts(b("eb"), b("m1e", 0, 8), 12, OP.logical_shift_right)
        ts(b("kk", 0, 8, key="kk0"), b("m1e", 0, 8), 7, OP.logical_shift_right, 31, OP.bitwise_and)
        ts(b("kq"), b("m2e", 0, 8), 7, OP.logical_shift_right, 31, OP.bitwise_and)
        to_q = b("pb1", 8, 16)
        mm(to_q, b("ex2", 0, 128), b("sb", 0, 8, key="sb0"), True, False)
        mm(to_q, b("ex2", 128, 256), b("sb", 8, 16, key="sb1"), False, True)
        scan(b("k0s"), b("RM", 0, 136), b("pb0", 272, 408), OP.max, OP.min)
        ts(b("qu"), to_q, 1600.0, OP.add)
        if s != 2:
            count("eqa", "nonr" if t == 1 else "one8", ("pb1", 16))
        tt(b("sm"), ind(b("A", 0, WIN), b("qu")), b("abm"), OP.add)
        if s == 0:
            consts_c()
        ym = b("pb2", 384, 512)
        ts(ym, b("sm"), 0.5, OP.mult, MAGIC, OP.add)
        tt(b("dM"), b("xs"), ym, OP.subtract)
        tt(b("pb1", 256, 384), b("pb1", 384, 512), b("am4"), OP.max)
        tt(b("hv"), b("pb1", 256, 384), b("ap4"), OP.min)

        less_x(0)
        act(b("bod"), ind(b("Tb", 0, WIN), b("bu")), AF.Copy)
        act(b("nrm"), b("k0s", 16, 136, 17), AF.Relu, -16.0)
        codes_masked("bod")
        act(b("absM"), b("dM"), AF.Abs)
        mm(b("pb1", 24, 32), b("absM"), b("selb"))
        gather(1)
        less_x(1)
        equal("bod", "pb3", 0)
        away(0)
        if s != 2:
            equal("bod", "pb4", 1)
        gather(2)
        act(b("Mb"), ym, AF.Identity, -MAGIC)
        away(1)
        gather(3)
        act(b("dvf"), ind(b("C", 0, WIN), b("bu")), AF.Copy)

        ac = b("gm3", 8, 16, key="ac")
        if s == 2:
            cp(ac, b("act0"))
        else:
            tt(ac, b("pb1", 16, 24), b("one8" if s == 0 else "nonr"), OP.is_lt)
        em = b("pb1", 24, 32)
        ah, am = b("gm3", 0, 8, key="ah"), b("gm3", 16, 24, key="am")
        tt(b("hm"), em, b("eb"), OP.min)
        tt(b("he"), em, b("eb"), OP.is_ge)
        tt(b("nn"), b("lim"), b("hm"), OP.is_lt)
        tt(b("T0"), b("lim1"), b("hm"), OP.min)
        tt(b("an"), b("nn"), ac, OP.mult)
        tt(b("Tt"), b("T0"), ac, OP.mult)
        tt(b("ah0"), ac, b("an"), OP.subtract)
        tt(b("k2"), b("an"), b("k0s", 16, 136, 17), OP.mult)
        tt(ah, b("ah0"), b("he"), OP.mult)
        tt(b("anr0"), b("an"), b("nrm"), OP.mult)
        tt(am, b("ah0"), ah, OP.subtract)
        if s == 0:
            cp(b("act0"), ac)
        tt(b("k1"), am, b("kk", 0, 8, key="kk0"), OP.mult)
        tt(b("kk", 16, 24, key="kk2"), am, b("kq"), OP.mult)
        tt(b("kk", 8, 16, key="kk1"), b("k1"), b("k2"), OP.add)
        tt(b("gm3", 24, 32, key="ax"), b("an"), b("anr0"), OP.subtract)
        tt(b("oh"), ind(b("kk", key=["kk0", "kk1", "kk2"]), bl(24)), b("kpat"), OP.is_equal)
        if s == 0:
            consts_d()
        ohb, ohn, ohe = b("oh", 0, 128), b("oh", 128, 256), b("oh", 256, 384)
        i8 = b("GE", 128, 256, key="GE1")
        mm(b("pb2", 256, 384), ohb, i8)
        mm(b("pb2", 0, 128), ohn, i8, True, False)
        mm(b("pb2", 0, 128), ohe, i8, False, True)
        mm(b("pb2", 128, 256), ohn, b("GN", 128 + 128 * s, 256 + 128 * s, key="GN%d" % s), True, False)
        mm(b("pb2", 128, 256), ohn, b("Di"), False, False)
        mm(b("pb2", 128, 256), ohe, b("m1c"), False, True)
        less_x(2)
        act(b("gx"), ind(b("gm3", 16, 32, key=["am", "ax"]), bl(16)), AF.Copy)
        away(2)
        if t == 1:
            send_rank()
        tt(b("gm"), ind(b("gm3", 0, 24, key=["ah", "ac", "am"]), bl(24)), b("rmask"), OP.mult)
        to_lists("gm", 3, ("pb1", 32), (2, 2, 2))
        if t == 1:
            to_lists("exP", 1, ("pb1", 80), (2,))
        mm(b("pb5", 0, 128), b("gx", 0, 128), b("idb"))
        mm(b("pb5", 128, 256), b("gx", 128, 256), b("idb"))
        less_x(3)
        sums2(0, 96, (0, 1, 2))
        away(3)
        sums2(96, 128, (3,))
        if s == 2:
            equal("bod", "pb4", 1)
        tt(b("w3"), b("cvf"), b("pb2", 256, 384), OP.max)
        tt(b("wal"), b("cvf"), b("pb2", 0, 128), OP.max)
        act(b("pb6", 0, 128), b("w3"), AF.Relu, 8 * 4095.0, -8.0)
        tt(b("ral"), b("wal"), b("pb2", 128, 256), OP.add)
        act(b("pb7", 0, 128), b("pb2", 0, 128), AF.Relu, 4095.0, -1.0)
        act(b("eqb", 0, 512, key="eqb0"), b("pb3"), AF.Relu, -10.0)
        act(b("eqb", 512, 1024, key="eqb1"), b("pb4"), AF.Relu, -10.0)
        tt(b("g3"), b("pb1", 32, 56), b("X3", key=["X3a", "X3b", "X3c"]), OP.mult)
        tt(b("pb5", 256, 384), b("pb5", 0, 128), b("Mb"), OP.mult)
        tt(b(tv, 8, 16, key=tv + "u"), b("g3", 8, 16), b("dmp"), OP.add)
        tt(b("t2"), b("pb5", 128, 256), b("xb"), OP.mult)
        cp(b("uvu"), b(tv, 8, 16, key=tv + "u"))
        tt(b("Dv", 0, 8, key="Dv0"), b("g3", 0, 8), b("g3", 16, 24), OP.add)
        scatter(b("C"), b("uvu"), b("ral"))
        if t == 1:
            send_list(s - 1)
        tt(b("pb5", 384, 512), b("pb6", 0, 128), b("dvf"), OP.add)
        tt(b("rsp"), b("w3"), b("pb5", 384, 512), OP.min)

        scan(b("fsm"), b("RM2"), b("pb0", 0, 128), OP.max, OP.min)
        tt(b("Sf"), b("fsm", 15, 128, 16), b("Tt"), OP.is_lt)
        act(b("exU"), ind(b("Sf"), bl(8)), AF.Copy)
        if t == 1:
            tt(b("ov"), b("Sf"), b("anr0"), OP.is_lt)
            ts(b("nov"), b("ov"), 0.0, OP.is_equal, b("p128"), OP.mult)
            mm(b("pb3", 8, 16), b("tri"), b("ov"))
        expand("exS", b("Sf"), 1)
        if t == 1:
            tt(b("pos"), b("pb3", 8, 16), b("nov"), OP.max)
            expand("exP", b("pos"), 1)
        tt(b("hF"), b("Sf"), ah, OP.is_lt)
        mm(b("pb1", 56, 64), one, b("onesb", 0, 8, 1, 0, 1), True, False)
        mm(b("pb1", 56, 64), b("exS"), b("sb", 0, 8, key="sb0"), False, True)
        mm(b("pb1", 64, 72), b("exS"), b("sb", 24, 32, key="sb3"))
        if t == 1:
            to_lists("exP", 1, ("pb1", 80), (2,))
            tt(b("An"), b("pb5", 256, 384), b("t2"), OP.add)
            tt(b("cb"), b("pb7", 0, 128), b("cvf"), OP.max)
            send_list(s)
        count("eqb", "hF", ("pb3", 0))
        if t == 0:
            tt(b("An"), b("pb5", 256, 384), b("t2"), OP.add)
            tt(b("cb"), b("pb7", 0, 128), b("cvf"), OP.max)
        tt(b("q1"), b("pb1", 56, 72), b("Dv", key=["Dv0", "Dv1"]), OP.mult)
        tt(b("vf", 0, 16, key="vf"), b("q1"), b(tv, 0, 16, key=[tv, tv + "u"]), OP.add)
        cp(b("vu2"), b("vf", 0, 16, key="vf"))
        scatter(b("CW", key="C"), b("vu2", 8, 16), b("rsp"))
        mm(b("pb2", 128, 256), b("exU"), b("GE", 128, 256, key="GE1"), True, False)
        mm(b("pb2", 128, 256), b("exU"), b("m1c"), False, True)
        mm(b("pb2", 0, 128), one, one, True, False)
        mm(b("pb2", 0, 128), b("exU"), b("m1c"), False, True)
        tt(b("h1"), b("pb3", 0, 8), b("hF"), OP.is_lt)
        expand("exH", b("h1"), 1)
        tt(b("C", n0, n0 + L), b("pb2", 128, 256), b("cb"), OP.max)
        to_lists("exH", 1, ("pb1", 72), (2,))
        if s == 3:
            dma("y", "ld5", T.yc[:], b("C", 0, W)[0], ["C"], ["yc"])
        tt(b("A", n0, n0 + L), b("pb2", 0, 128), b("An"), OP.mult)
        tt(b("oA"), b("pb1", 72, 80), b("bd"), OP.mult)
        if s < 3:
            front_v(s + 1, b("tu") if s == 1 else b("vu2", 0, 8))
        tt(b("oA"), b("oA"), b("dmp"), OP.add)
        if t == 1:
            tt(b("nF"), b("Sf"), b("an"), OP.is_lt)
        cp(b("oAu"), b("oA"))
        scatter(b("A"), b("oAu"), b("hv"))
        if s == 3:
            dma("y", "ld6", T.ya[:], b("A", 0, W)[0], ["A"], ["ya"])
        if t == 1:
            tt(b("rest2"), b("rest"), b("nF"), OP.add)
            act(b("nonr2"), b("rest2"), AF.Identity, 1.0, -1.0)

    def send_rank():
        tt(b("pos"), b("pb1", 96, 104), b("nov"), OP.max)
        expand("exP", b("pos"), 1)

    def send_list(s):
        h = hops(T, topo, rank, s)
        m = "msg%d" % s
        cp(b("posu"), b("pb1", 80, 88))
        scatter(b(m), b("posu"), b("xp"))
        need("g", [m], [])
        n = engines_of(topo, core, h[1])
        rid, pid = topo.addr(h[1], core)
        if len(h) == 3:
            to, sem = T["rl%d" % s][:, 0:CAP], T.sem["rr%d" % s]
        else:
            to, sem = T["come%d" % (s // ST)][:, CAP * (s % ST):CAP * (s % ST) + CAP], T.sem["in%d" % s]
        g.remote_dma(to, T[m][:, 0:CAP], sem, T.sem["ls%d" % s], pid, rid, emask(topo, core, h[1], n))

    for s in range(ST * RO):
        h = hops(T, topo, (rank - 1 - s % (NR - 1)) % NR, s)
        n = engines_of(topo, h[-2], h[-1])
        wr["come%d_%d" % (s // ST, s % ST)] = ("remote", "in%d" % s, n, {"in%d" % s: n})
        cnt["in%d" % s] = n

    def round_end(s):
        cm = "come%d" % (s // ST)
        mm(b("pb3", 16, 24), b("tri"), b("rest2"), True, False)
        mm(b("pb3", 16, 24), b("I128"), b("nonr2"), False, True)
        tt(b("dM"), ind(b("A", 0, WIN), b("vu2", 0, 8)), b("xb"), OP.subtract)
        act(b("ad"), b("dM"), AF.Abs)
        cp(b("nrs"), b("pb3", 16, 24))
        expand("exN", b("nrs"), 1)
        to_lists("exN", 1, ("pb1", 88), (2,))
        if s == 1:
            front(2, b("tu"))
            act(b("cvf"), ind(b("C", 0, WIN), b("tu")), AF.Copy)
            for c in range(4):
                o, a = b("ag", 512 * c, 512 * c + 512, key="ag%d" % c), ind(b("A", 0, WIN), b("cvu", 32 * c, 32 * c + 32))
                if c < 3:
                    act(o, a, AF.Copy)
                else:
                    cp(o, a)
        ts(b("msk"), b(cm, 0, CAP, key=cm + "_0"), 0.5, OP.is_gt)
        op("v", lambda e: e.tensor_reduce(b("n0")[0], b("msk")[0], AxisListType.X, OP.add), ["msk"], ["n0"])
        ts(b("cd"), b("n0"), -1.0, OP.mult, float(CAP), OP.add)
        ts(b("ge"), b("pb1", 88, 96), b("n0"), OP.is_ge, b("cd"), OP.mult)
        tt(b("idx"), b("pb1", 88, 96), b("ge"), OP.add)
        ts(b("iu"), b("idx"), 64.0, OP.min)
        tt(b("hx"), ind(b(cm, key=[cm + "_0", cm + "_1", cm + "z"]), b("iu")), b("ad"), OP.max)
        ts(b("xi"), b("hx"), 255, OP.bitwise_and)

    for s in range(4):
        if s % ST == 0:
            step(s, b("tu"), "topf")
        else:
            step(s, b("vu2", 0, 8), "vf")
            round_end(s)
    cp(b("xb"), b("xi"))
    dma("y", "ld7", T.yx[:], b("xb")[0], ["xb"], ["yx"])
    for n in sorted(cnt):
        if cnt[n] and know["g"].get(n, 0) < cnt[n]:
            g.wait_ge(T.sem[n], cnt[n])
    for s in range(4):
        g.wait_ge(T.sem["ls%d" % s], engines_of(topo, core, hops(T, topo, rank, s)[1]))
